import numpy as np, ml_dtypes
CORES = [35,38,43,46]
N = 4
BF = ml_dtypes.bfloat16
W, M, C, R, P = 4096, 2048, 256, 3, 1
def accounts(rng):
    H = W // 2; k = np.stack([rng.permutation(H) for _ in range(8)]); pw = rng.choice(np.array([1.0, 1.5, 2.0]), 8)
    c = np.minimum((H * rng.random((N, 8, 16 * M)) ** pw[None, :, None]).astype(np.int64), H - 1)
    e = (2 * k[np.arange(8)[None, :, None], c] + rng.integers(0, 2, c.shape)).reshape(N, 8, 16, M)
    none = (rng.random((N, 8, 16, M)) < 0.6 * rng.random((N, 8, 1, M)) ** 2) | (rng.random((N, 8, 1, M)) < 0.01)
    return np.where(none, W, e)
def keeps(rng):
    return rng.choice(np.array([0.0, 0.1, 0.3, 0.8]), (N, 8, 1, W // 2))
def books(rng, acct, keep):
    H = W // 2; out = rng.integers(0, M, (N, 8, 16, H)); m = np.tile(np.arange(M), 16)
    for q in range(N):
        for g in range(8):
            o = rng.permutation(16 * M); c = acct[q, g].reshape(-1)[o] >> 1
            s = np.argsort(c, kind="stable"); c = c[s]; who = m[o[s]]
            pos = np.arange(16 * M) - np.searchsorted(c, c)
            ok = (pos < 16) & (c < H) & (rng.random(16 * M) < keep[q, g, 0][np.minimum(c, H - 1)])
            out[q, g, pos[ok], c[ok]] = who[ok]
    return np.take_along_axis(out, np.argsort(rng.random(out.shape), axis=2), 2)
def losses(rng):
    return np.clip(np.rint(90 * rng.standard_normal((N, 8, 16, W), dtype=np.float32)), -255, 255).astype(np.int64)
def tops(loss, acct):
    x = np.take_along_axis(np.concatenate([loss, np.zeros((N, 8, 16, 1), np.int64)], axis=3), acct[..., :R * C].reshape(N, 8, 1, -1), 3)
    return np.max(np.add.reduce(x.reshape(N, 8, 16, 16, R * C), axis=3), axis=2)
def pack(loss, acct, book, cap):
    return {"loss": np.ascontiguousarray(loss.reshape(N, 128, W)).astype(np.float32).astype(BF), "acct": np.ascontiguousarray(acct.reshape(N, 128, M)).astype(np.int32),
            "book": np.ascontiguousarray(book.reshape(N, 128, W // 2)).astype(np.int32), "cap": np.ascontiguousarray(cap).astype(np.int32)}
def setup_inputs(rng):
    acct = accounts(rng)
    return pack(losses(rng), acct, books(rng, acct, keeps(rng)), rng.integers(0, 900, (N, 8, R * C)))
def setup_inputs_ties(rng):
    acct = accounts(rng); acct[:, ::2, 8:12] = acct[:, ::2, 0:4]
    loss = rng.integers(-2, 3, (N, 8, 16, W)) * rng.choice(np.array([1, 3, 100]), (N, 8, 1, 1)); loss[:, 1::2, 8:] = loss[:, 1::2, :8]
    loss[:, 6] = rng.integers(180, 255, (N, 1, 1)) + rng.integers(-1, 2, (N, 16, W))
    cap = np.clip(tops(loss, acct) + rng.choice(np.array([-1, -1, 0, 1]), (N, 8, R * C)), 0, 4095)
    keep = keeps(rng); keep[:, 6] = 0.8
    return pack(loss, acct, books(rng, acct, keep), cap)
def setup_inputs_crowd(rng):
    H = W // 2; acct = accounts(rng); loss = losses(rng); cap = rng.integers(0, 900, (N, 8, R * C))
    acct[:, 2:4] = 2 * rng.permutation(H)[:64][rng.integers(0, 64, (N, 2, 16, M))] + rng.integers(0, 2, (N, 2, 16, M))
    loss[:, :2] = rng.integers(-15, 16, (N, 2, 16, W)); cap[:, :2] = 0
    x = [int(2 * rng.integers(0, H)), int(2 * rng.integers(0, H) + 1)]; y = np.zeros((N, 2, 16), np.int64)
    for g in range(2):
        loss[:, g, :, x[g]] = 255
        for q in range(N):
            y[q, g] = R * C + rng.permutation(M - R * C)[:16]
            acct[q, g, rng.integers(0, 16, R * C), np.arange(R * C)] = x[g]
            acct[q, g, rng.integers(0, 16, 16), y[q, g]] = x[g] ^ 1
            acct[q, g, :, y[q, g, 1]] = x[g] ^ 1
    k = rng.permutation(H); e = 2 * k[:R * C] + rng.integers(0, 2, R * C); v = np.zeros((N, R * C), np.int64)
    acct[:, 4] = np.where(acct[:, 4] == W, W, 2 * k[rng.integers(R * C, H, (N, 16, M))] + rng.integers(0, 2, (N, 16, M)))
    big = rng.integers(-15, 16, (N, 16, W)); big[:, :, e] = rng.integers(240, 256, (N, 16, R * C)); loss[:, 4] = big; cap[:, 4] = 0
    for q in range(N):
        v[q] = R * C + rng.permutation(M - R * C)[:R * C]
        acct[q, 4, rng.integers(0, 16, R * C), np.arange(R * C)] = e
        acct[q, 4, rng.integers(0, 16, R * C), v[q]] = e ^ 1
    book = books(rng, acct, keeps(rng))
    for g in range(2):
        for q in range(N):
            book[q, g, :, x[g] >> 1] = y[q, g]; book[q, g, 0, x[g] >> 1] = rng.integers(0, R * C)
    for q in range(N): book[q, 4, rng.integers(0, 16, R * C), e >> 1] = v[q]
    return pack(loss, acct, book, cap)
def setup_inputs_ends(rng):
    H = W // 2; acct = accounts(rng); loss = losses(rng); cap = rng.integers(0, 300, (N, 8, R * C))
    acct[:, 0] = rng.choice(np.array([0, 1, W - 2, W - 1, W]), (N, 16, M))
    acct[:, 1, :, ::2] = acct[:, 1, :1, ::2]
    acct[:, 2:4, :, M - 1] = W
    acct[:, 4] = 2 * (rng.integers(-16, 16, (N, 16, M)) % H) + rng.integers(0, 2, (N, 16, M))
    acct[:, 5, 1:] = W
    acct[:, 6] = np.where(acct[:, 6] == W, rng.integers(0, W, (N, 16, M)), acct[:, 6]); loss[:, 6, 15] = 255
    cap[:, 6] = rng.choice(np.array([0, 4079, 4080, 4095]), (N, R * C))
    loss[:, 7, 1:] = -255
    book = books(rng, acct, np.full((N, 8, 1, H), 0.8))
    book[:, 2:4, :15] = M - 1
    book[:, 4] = rng.choice(np.array([0, M - 1, C - 1, C]), (N, 16, H))
    return pack(loss, acct, book, cap)
def setup_inputs_quiet(rng):
    acct = accounts(rng); cap = rng.integers(0, 900, (N, 8, R * C)); keep = keeps(rng); q = rng.permutation(N); g = rng.permutation(8)
    cap[q[0]] = 4095; cap[q[0], g[0]] = rng.integers(0, 300, R * C); cap[q[1]] = 0; cap[:, g[1]] = 4095
    keep[q[2]] = 0.0; keep[q[3]] = 1.0
    return pack(losses(rng), acct, books(rng, acct, keep), cap)
def setup_inputs_spread(rng):
    acct = rng.integers(0, W + 1, (N, 8, 16, M))
    loss = np.clip(np.rint(rng.standard_normal((N, 8, 16, W)) * np.exp2(rng.integers(0, 9, (N, 8, 1, W))) * (rng.random((N, 8, 1, W)) > 0.0625)), -255, 255).astype(np.int64)
    cap = np.exp2(12 * rng.random((N, 8, R * C))).astype(np.int64) - 1
    return pack(loss, acct, books(rng, acct, rng.random((N, 8, 1, W // 2))), cap)
def check_inputs(d):
    bad = []; v = np.asarray(d["loss"]).astype(np.float32)
    if not np.all((v >= -255) & (v <= 255) & (v == np.rint(v))): bad.append("whole numbers of loss")
    for k, hi in (("acct", W), ("book", M - 1), ("cap", 4095)):
        if np.min(d[k]) < 0 or np.max(d[k]) > hi: bad.append("range of " + k)
    return bad
def reference(loss, acct, book, cap):
    L = loss.astype(np.float32).astype(np.int64).reshape(N, 8, 16, W)
    L = np.concatenate([L, np.zeros((N, 8, 16, 1), np.int64)], axis=3)
    A = acct.astype(np.int64).reshape(N, 8, 16, M); B = book.astype(np.int64).reshape(N, 8, 16, W // 2); K = cap.astype(np.int64)
    said = np.zeros((N, 8, R * C), np.float32); slot = np.arange(C); rank = np.arange(N)[:, None]
    for t in range(R):
        lo = C * t
        mine = np.ascontiguousarray(A[..., lo:lo + C])
        x = np.take_along_axis(L, mine.reshape(N, 8, 1, 16 * C), 3).reshape(N, 8, 16, 16, C)
        z = np.add.reduce(x, axis=3)
        w = np.argmax(z, axis=2)
        over = np.max(z, axis=2) > K[..., lo:lo + C]
        xw = np.take_along_axis(x, w[:, :, None, None, :], 2)[:, :, 0]
        i = np.argmax(xw, axis=2)
        e = np.take_along_axis(mine, i[:, :, None], 2)[:, :, 0]
        d = 1 + (P * t + slot // (C // P)) % (N - 1)
        src = (rank - d) % N
        ok = over[src, :, slot].transpose(0, 2, 1)
        eo = np.where(ok, e[src, :, slot].transpose(0, 2, 1), 0); opp = eo ^ 1
        cand = np.take_along_axis(B, (eo >> 1)[:, :, None], 3)
        held = np.take_along_axis(A, cand.reshape(N, 8, 1, 16 * C), 3).reshape(N, 8, 16, 16, C)
        holds = np.any(held == opp[:, :, None, None], axis=2)
        found = ok & np.any(holds, axis=2)
        h = np.take_along_axis(cand, np.argmax(holds, axis=2)[:, :, None], 2)[:, :, 0]
        h = np.where(found, h, M + slot)
        same = (h[..., :, None] == h[..., None, :]) & (slot[None, :] < slot[:, None])
        acc = found & ~np.any(same, axis=-1)
        col = np.take_along_axis(A, np.where(acc, h, 0)[:, :, None], 3); new = np.where(col == opp[:, :, None], W, col)
        A = np.concatenate([A, np.zeros((N, 8, 16, C), np.int64)], axis=3)
        np.put_along_axis(A, np.ascontiguousarray(np.broadcast_to(np.where(acc, h, M + slot)[:, :, None], new.shape)), new, 3)
        A = np.ascontiguousarray(A[..., :M])
        back = acc[(rank + d) % N, :, slot].transpose(0, 2, 1)
        hit = back[:, :, None] & (np.arange(16)[None, None, :, None] == i[:, :, None])
        A[..., lo:lo + C] = np.where(hit, W, A[..., lo:lo + C])
        said[..., lo:lo + C] = over.astype(np.int64) + back.astype(np.int64)
    return {"left": (A < W).reshape(N, 128, M).astype(np.float32).astype(BF), "said": said}

@@ -1,0 +1,422 @@
+from concourse.mybir import AluOpType as A, ActivationFunctionType as F
+
+
+def _bufs(where, dtype, spec):
+    return {n: (where, [128] + list(sh), dtype) for names, sh in spec for n in names.split()}
+
+
+SCRATCH = {}
+SCRATCH.update(_bufs("sbuf", "float32", [
+    ("capF offS seg colf ZT M1 PIE K2E cn oppB Lo P1 cZ xs e4 kL Q1 Q2", [256]), ("capT ov sd", [768]), ("Z DF", [2320]),
+    ("W", [4104]), ("rep", [4096]), ("pF pm0 dum", [16]), ("dif If", [128]), ("Pf", [512]), ("d17 S2 dE E cTP", [272]), ("u17 s1 s2 Woh", [17]),
+    ("Of4", [24, 2, 16])]))
+SCRATCH.update(_bufs("sbuf", "bfloat16", [
+    ("L", [4112]), ("LF Wacc eqd", [2320]), ("X0 X1 eq", [4096]), ("XT", [4128]), ("DFb", [24, 2, 16]), ("Iz BO b1", [128]),
+    ("Pb", [512]), ("cst", [544]), ("Fv f1", [8, 32]), ("Fj", [2048]), ("eqm cL LFo ohb accb", [256])]))
+SCRATCH.update(_bufs("sbuf", "float16", [("NBO", [128]), ("h16", [272]), ("P2", [16, 17])]))
+SCRATCH.update(_bufs("sbuf", "int32", [("Ai", [2320]), ("Bi", [2064]), ("capN", [768]), ("nA", [256]), ("pI", [8]), ("k1 k2 KI iI", [16]), ("EI", [32])]))
+SCRATCH.update(_bufs("sbuf", "uint16", [("tile", [768]), ("prm o1 iT hT oL", [16]), ("colc cand", [256]), ("msg mins", [96]), ("rin rout", [48])]))
+SCRATCH.update(_bufs("psum", "float32", [("zp pie0 pie1", [16, 2, 16]), ("valA valB hA hB TP", [512])]))
+DMAS = ["dA0", "dL", "dcap", "dcap1", "dA1", "dA2", "dB", "dO0", "dO1", "dO2", "dS0", "dS1"]
+SEMAPHORES = ["sV", "sS", "sP", "sG", "sent", "arr0", "arr1", "arr2", "rep0", "rep1", "rep2"] + DMAS
+PSUM = ("zp", "pie0", "pie1", "valA", "valB", "hA", "hB", "TP")
+XS = -131072.0
+NOOFF = 127.0 * 131072.0 - 4096.0
+
+
+def rank_program(g, core, T, topo):
+    rank = T.rank_of(core)
+    if rank is None:
+        return
+    N = len(T.cores)
+    Q = {"V": g.vector, "S": g.scalar, "P": g.tensor, "G": g, "Y": g.sync}
+    ops, lastw, readers = [], {}, {}
+
+    def op(eng, fn, r="", w="", sem=None, cnt=0):
+        r, w = r.split(), w.split()
+        w += [x for x in r if x in PSUM]
+        deps = set(lastw[x] for x in r + w if x in lastw)
+        for x in w:
+            deps.update(readers.get(x, ()))
+        if eng == "P":
+            deps = set(d for d in deps if ops[d]["eng"] != "P")
+        ops.append({"eng": eng, "fn": fn, "deps": deps, "sem": sem, "cnt": cnt, "need": False, "waits": []})
+        for x in r:
+            readers.setdefault(x, []).append(len(ops) - 1)
+        for x in w:
+            lastw[x] = len(ops) - 1
+            readers[x] = []
+
+    def dma(eng, sem, out, in_, r="", w=""): op(eng, lambda q: q.dma_start(out, in_), r, w, sem, 16)
+    def ts(out, a, x, o0, r, w): op("V", lambda q: q.tensor_scalar(out, a, x, None, o0), r, w)
+    def ts2(out, a, x, y, o0, o1, r, w): op("V", lambda q: q.tensor_scalar(out, a, x, y, o0, o1), r, w)
+    def tt(out, a, b, o, r, w): op("V", lambda q: q.tensor_tensor(out, a, b, o), r, w)
+    def cp(out, a, r, w): op("V", lambda q: q.tensor_copy(out, a), r, w)
+    def tr(out, a, r, w): op("V", lambda q: q.transpose(out, a), r, w)
+    def ms(out, c, w): op("V", lambda q: q.memset(out, c), "", w)
+    def scan(out, d0, d1, init, o0, o1, r, w): op("V", lambda q: q.tensor_tensor_scan(out, d0, d1, init, o0, o1), r, w)
+    def act(out, a, f, r, w, bias=0.0, scale=1.0): op("S", lambda q: q.activation(out, a, f, bias=bias, scale=scale), r, w)
+    def mm(out, l, rhs, st, sp, r, w): op("P", lambda q: q.matmul(out, l, rhs, st, sp), r, w)
+    def iota(out, pat, base, cm, w): op("G", lambda q: q.iota(out, pat, base, cm, allow_small_or_imprecise_dtypes=True), "", w)
+    def sel(out, a, pat, cmp, fill, base, cm, r, w): op("G", lambda q: q.affine_select(out, a, pat, cmp, fill, base, cm), r, w)
+
+    sent = [0]
+
+    def send(out, in_, sem, peer, r):
+        rid, pid, _ = topo.addr(peer)
+        es = topo.engines(core, peer)[:8]
+        sent[0] += len(es)
+        op("G", lambda q: q.remote_dma(out, in_, T.sem[sem], T.sem.sent, pid, rid, sum(1 << e for e in es)), r, "", "remote")
+
+    def arrive(name, sem, peer):
+        op("X", None, "", name, sem, len(topo.engines(peer, core)[:8]))
+
+    Xb, Xn = [T.X0, T.X1, T.X0], ["X0", "X1", "X0"]
+    pie = [T.pie0, T.pie1]
+    Aall = " A0 A1 A2 Apad "
+    def col(j): return T.pF[:, j:j + 1]
+    def rng(t): return slice(256 * t, 256 * t + 256)
+    def An(t): return " A%d " % min(t, 1)
+    def Xu(t, u, n): return " " + " ".join("%s_%d" % (Xn[t], k) for k in range(u, u + n))
+
+    dma("Y", "dA0", T.Ai[:, 0:256], T.acct[:, 0:256], "", "A0")
+    ms(T.capN[:, 0:256], 0, "capN0")
+    dma("Y", "dcap", T.capN[0:128:16, 0:256], T.cap[:, 0:256], "", "capN0")
+    dma("Y", "dL", T.L[:, 0:4096], T.loss[:, :], "", "L")
+    ms(T.capN[:, 256:768], 0, "capN1")
+    dma("Y", "dA1", T.Ai[:, 256:768], T.acct[:, 256:768], "L", "A1")
+    dma("Y", "dcap1", T.capN[0:128:16, 256:768], T.cap[:, 256:768], "", "capN1")
+    dma("Y", "dB", T.Bi[:, 0:2048], T.book[:, :], "", "B")
+    dma("Y", "dA2", T.Ai[:, 768:2048], T.acct[:, 768:2048], "", "A2")
+
+    op("G", lambda q: q.iota(T.pI[:, 0:1], [[0, 1]], 0, 1), "", "pI0")
+    iota(T.pm0[:, :], [[32, 8], [8, 2]], 0, 0, "pm0")
+    iota(T.dif[:, :], [[-1, 128]], 0, 1, "dif")
+    iota(T.offS[:, 0:128], [[512, 4], [0, 2], [32, 16]], 0, 0, "offS")
+    iota(T.f1[:, :, :], [[0, 256]], -131072, 0, "f1")
+    sel(T.Fv[:, :, :], T.f1[:, :, :], [[0, 8], [1, 32]], A.is_gt, 0.0, -15, 0, "f1", "Fv")
+    sel(T.Fv[:, :, :], T.Fv[:, :, :], [[0, 8], [1, 32]], A.not_equal, 4096.0, -15, 0, "Fv", "Fv")
+    sel(T.Fv[:, :, :], T.Fv[:, :, :], [[-16, 8], [0, 32]], A.is_ge, 0.0, 0, 1, "Fv", "Fv")
+    sel(T.Fv[:, :, :], T.Fv[:, :, :], [[16, 8], [0, 32]], A.is_ge, 0.0, 15, -1, "Fv", "Fv")
+    iota(T.u17[:, :], [[1, 17]], 0, 0, "u17")
+    iota(T.dum[:, :], [[16, 16]], 2049, 0, "dum")
+    iota(T.colf[:, :], [[1, 256]], 0, 0, "colf")
+    iota(T.b1[:, :], [[0, 128]], 4096, 0, "b1")
+    sel(T.BO[:, :], T.b1[:, :], [[-16, 8], [0, 16]], A.is_ge, 0.0, 0, 1, "b1", "BO")
+    sel(T.BO[:, :], T.BO[:, :], [[16, 8], [0, 16]], A.is_ge, 0.0, 15, -1, "BO", "BO")
+    iota(T.W[:, 0:256], [[2, 128], [-1, 2]], 1, 0, "W")
+    iota(T.W[:, 1024:4104], [[2, 1540], [-1, 2]], 1025, 0, "W1")
+
+    ms(T.seg[:, :], 0.0, "seg")
+    ms(T.seg[:, 0:256:16], 2.0 ** 27, "seg")
+    ms(T.LF[:, 2048:2320], 0.0, "LF")
+    ms(T.L[:, 4096:4112], 0.0, "Lpad")
+    ms(T.XT[:, 2048:2064], 0.0, "XTpad0")
+    ms(T.XT[:, 4112:4128], 0.0, "XTpad1")
+    for j in (1, 2):
+        act(T.DF[:, rng(j)], T.seg[:, :], F.Sigmoid, "seg", "DF", -1000.0, 0.0)
+    for j in range(16):
+        act(T.Fj[:, 128 * j:128 * j + 128], T.Fv[:, :, 15 - j:31 - j], F.Copy, "Fv", "Fj%d" % j)
+    lastw["Fj"] = lastw["Fj15"]
+    p0 = T.pI[:, 0:1]
+    ts(T.pI[:, 1:2], p0, 15, A.bitwise_and, "pI0", "pI1")
+    ts(T.pI[:, 2:3], p0, 31, A.bitwise_and, "pI0", "pI2")
+    ts2(T.pI[:, 3:4], p0, 4, 1, A.arith_shift_right, A.bitwise_and, "pI0", "pI3")
+    ts(T.pI[:, 4:5], p0, 1, A.bitwise_and, "pI0", "pI4")
+    ts2(T.pI[:, 5:6], p0, 1, 7, A.arith_shift_right, A.bitwise_and, "pI0", "pI5")
+    cp(T.pF[:, 0:6], T.pI[:, 0:6], "pI0 pI1 pI2 pI3 pI4 pI5", "pF")
+    ts2(col(7), col(4), 16.0, col(5), A.mult, A.add, "pF", "c7")
+    ts2(col(8), col(3), -1.0, 1.0, A.mult, A.add, "pF", "c8")
+    ts2(col(9), col(1), 8192.0, 127.0 * 131072.0, A.mult, A.add, "pF", "c9")
+    ts(T.prm[:, :], T.pm0[:, :], col(7), A.add, "pm0 c7", "prm")
+
+    def prep_tile(t):
+        cp(T.tile[:, rng(t)], T.Ai[:, rng(t)].indirect(T.prm[:, :]), An(t) + "prm", "tile%d" % t)
+
+    def prep_pos(t):
+        cp(T.Of4[:, 8 * t:8 * t + 8], T.Ai[:, rng(t)], An(t), "Of%d" % t)
+
+    def prep_cap(t):
+        ts2(T.capF[:, :], T.capN[:, rng(t)], -4096.0, -2048.0, A.mult, A.add, "capN%d" % min(t, 1), "capF")
+        tr(T.capT[:, rng(t)], T.capF[:, :], "capF", "capT%d" % t)
+
+    def swap(l, r, rhs4, b0, h, st, sp):
+        for k in range(4):
+            mm(pie[h][:, 0:4, k // 2, :], l[:, 128 * k:128 * k + 128], rhs4[:, b0 + 4 * h:b0 + 4 * h + 4, k % 2, :], st and k == 0, sp and k == 3, r, "pie%d" % h)
+
+    def evac(h):
+        act(T.PIE[:, 128 * h:128 * h + 128], pie[h][:, 0:4], F.Identity, "pie%d c9" % h, "PIE%d" % h, col(9))
+
+    def gx(eng, t, u, n):
+        out = Xb[t][:, 512 * u:512 * (u + n)]
+        src = T.L[:, :].indirect(T.tile[:, 256 * t + 32 * u:256 * t + 32 * (u + n)])
+        r = "L Lpad tile%d" % t
+        if eng == "V": ts(out, src, XS, A.mult, r, Xu(t, u, n))
+        else: act(out, src, F.Copy, r, Xu(t, u, n), 0.0, XS)
+
+    def tx(t, p):
+        o = 1024 * p + (16 if p >= 2 else 0)
+        tr(T.XT[:, o:o + 1024], Xb[t][:, 1024 * p:1024 * p + 1024], Xu(t, 2 * p, 2), "XT%d" % p)
+
+    def zmm(t, h):
+        if h == 0:
+            mm(T.zp[:, 0:8], T.If[:, :], T.offS[:, :], True, False, "If offS", "zp")
+        for k in range(32):
+            mm(T.zp[:, 4 * h:4 * h + 4, k // 16, :], T.Iz[:, :], Xb[t][:, 2048 * h + k:2048 * h + 2048:32], False, h == 1 and k == 31, "Iz" + Xu(t, 4 * h, 4), "zp")
+
+    def consts_b():
+        ts(T.Woh[:, :], T.u17[:, :], col(1), A.is_equal, "u17 pF", "Woh")
+        ts2(T.s1[:, :], T.u17[:, :], col(1), 1.0, A.subtract, A.is_equal, "u17 pF", "s1")
+        ts2(T.d17[:, 16:17], col(1), 15.0, 2.0 ** 22, A.is_lt, A.mult, "pF", "d17a")
+        ts(T.s2[:, :], T.Woh[:, :], -2.0, A.mult, "Woh", "s2")
+        tt(T.d17[:, 17:33], T.Woh[:, 0:16], T.s1[:, 0:16], A.subtract, "Woh s1", "d17b")
+        tt(T.dE[:, 17:34], T.s1[:, :], T.s2[:, :], A.add, "s1 s2", "dE1")
+        ts(T.d17[:, 0:16], T.d17[:, 17:33], 2.0 ** 22, A.mult, "d17a d17b", "d17 d17b")
+        ts(T.dE[:, 0:17], T.dE[:, 17:34], 4096.0, A.mult, "dE1", "dE dE1")
+        ms(T.cTP[:, :], 2048.0, "cTP")
+        ms(T.P2[:, :, 16], 0.0, "P2pad")
+        ts(T.cTP[:, 16:272:17], T.dum[:, :], col(1), A.add, "dum pF", "cTP")
+
+    def consts_c():
+        for n in (1, 2, 4, 8):
+            act(T.dE[:, 17 * n:34 * n], T.dE[:, 0:17 * n], F.Copy, "dE", "dE")
+            act(T.d17[:, 17 * n:34 * n], T.d17[:, 0:17 * n], F.Copy, "d17", "d17")
+        act(T.Pb[:, :], T.Pf[:, :], F.Copy, "Pf0 Pf1 Pf2 Pf3", "Pb", 0.0, 2.0 ** 26)
+
+    def offers(t, src, sn):
+        tr(T.ZT[:, :], src, sn, "ZT")
+        scan(T.M1[:, :], T.seg[:, :], T.ZT[:, :], 0.0, A.add, A.min, "seg ZT", "M1")
+        tt(T.k1[:, :], T.M1[:, 15:256:16], T.capT[:, 256 * t:256 * t + 256:16], A.min, "M1 capT%d" % t, "k1")
+        ts(T.k2[:, :], T.k1[:, :], 4095, A.bitwise_and, "k1", "k2")
+        cp(T.o1[:, :], T.k2[:, :], "k2", "o1")
+        for h in range(2):
+            tt(T.K2E[:, 128 * h:128 * h + 128], T.XT[:, 2064 * h:2064 * h + 2064].indirect(T.o1[:, 8 * h:8 * h + 8]), T.PIE[:, 128 * h:128 * h + 128], A.add,
+               "XT%d XT%d XTpad%d o1 PIE%d" % (2 * h, 2 * h + 1, h, h), "K2E%d" % h)
+        tr(T.ZT[:, :], T.K2E[:, :], "K2E0 K2E1", "ZT")
+        scan(T.M1[:, :], T.seg[:, :], T.ZT[:, :], 0.0, A.add, A.min, "seg ZT", "M1")
+        ts(T.KI[:, :], T.M1[:, 15:256:16], NOOFF, A.min, "M1", "KI")
+        ts(T.EI[:, 0:16], T.KI[:, :], 8191, A.bitwise_and, "KI", "EI0")
+        ts2(T.EI[:, 16:32], T.KI[:, :], 8191, 1, A.bitwise_and, A.arith_shift_right, "KI", "EI1")
+        m = T.msg[:, 32 * t:32 * t + 32]
+        cp(m, T.EI[:, :], "EI0 EI1", "msg%d" % t)
+        send(T.mins[:, 32 * t:32 * t + 32], m, "arr%d" % t, T.cores[(rank + t + 1) % N], "msg%d" % t)
+        ts2(T.iI[:, :], T.KI[:, :], 13, 15, A.arith_shift_right, A.bitwise_and, "KI", "iI")
+        cp(T.iT[:, :], T.iI[:, :], "iI", "iT")
+
+    def own(t):
+        if t < 2: act(T.ohb[:, :], T.Woh[:, 0:16].indirect(T.iT[:, :]), F.Identity, "Woh iT", "ohb", XS, -XS)
+        else: act(T.Q1[:, :], T.Woh[:, 0:16].indirect(T.iT[:, :]), F.Identity, "Woh iT", "Q1", 2.0, -1.0)
+        act(T.ov[:, rng(t)], T.W[:, :].indirect(T.msg[:, 32 * t:32 * t + 16]), F.Sign, "W W1 msg%d" % t, "ov%d" % t, 4097.0, -1.0)
+
+    def acc(t): return T.Wacc[:, :].indirect(T.rin[:, 16 * t:16 * t + 16])
+
+    def answer(t):
+        arrive("rin%d" % t, "rep%d" % t, T.cores[(rank + t + 1) % N])
+        if t < 2:
+            act(T.accb[:, :], acc(t), F.Copy, "Wacc rin%d" % t, "accb", 0.0, -XS)
+            mm(T.valB[:, 0:256], T.Iz[:, :], T.ohb[:, :], True, False, "Iz ohb", "valB")
+            mm(T.valB[:, 0:256], T.Iz[:, :], T.accb[:, :], False, True, "Iz accb", "valB")
+        else:
+            tt(T.LFo[:, :], acc(t), T.Q2[:, :], A.is_lt, "Wacc rin2 Q2", "LFo")
+            dma("Y", "dO2", T.left[:, rng(t)], T.LFo[:, :], "LFo")
+
+    def taken(t):
+        tt(T.Ai[:, rng(t)], T.Ai[:, rng(t)], T.valB[:, 0:256], A.max, "valB" + An(t), An(t))
+
+    def said(t):
+        tt(T.sd[:, rng(t)], acc(t), T.ov[:, rng(t)], A.add, "Wacc rin%d ov%d" % (t, t), "sd%d" % t)
+
+    def verdict(t, fill_rep, fill_val, fill_s, fill_s2):
+        mm(T.hA[:, 0:272], T.BO[:, :], T.cst[:, 0:272], True, False, "BO cst", "hA")
+        mm(T.hB[:, 0:272], T.BO[:, :], T.cst[:, 272:544], True, False, "BO cst", "hB")
+        mm(T.TP[:, 0:272], T.If[:, :], T.cTP[:, :], True, False, "If cTP", "TP")
+        mn = " min%d " % t
+        arrive(mn, "arr%d" % t, T.cores[(rank - t - 1) % N])
+        oT, kT = T.mins[:, 32 * t:32 * t + 16], T.mins[:, 32 * t + 16:32 * t + 32]
+        cp(T.cand[:, :], T.Bi[:, :].indirect(kT), "B Bpad" + mn, "cand")
+        act(T.oppB[:, :], T.W[:, :].indirect(oT), F.Copy, "W W1" + mn, "oppB")
+        ts2(T.cn[:, :], T.cand[:, :], -1.0, 2048.0, A.mult, A.add, "cand", "cn")
+        fill_rep()
+        for k in range(8):
+            e = slice(512 * k, 512 * k + 512)
+            act(T.rep[:, e], T.oppB[:, :].indirect(T.colc[:, 32 * k:32 * k + 32]), F.Copy, "oppB colc", "rep%d" % k)
+            tt(T.eq[:, e], T.Ai[:, :].indirect(T.cand[:, 32 * k:32 * k + 32]), T.rep[:, e], A.is_equal, Aall + "cand rep%d" % k, "eq%d" % k)
+            if k % 2:
+                b = k // 2
+                for j in range(16):
+                    mm((T.valB if b == 3 else T.valA)[:, 64 * b:64 * b + 64], T.Fj[:, 128 * j:128 * j + 128], T.eq[:, 1024 * b + j:1024 * b + 1024:16],
+                       j == 0, j == 15, "Fj eq%d eq%d" % (k - 1, k), "valB" if b == 3 else "valA")
+        fill_s()
+        for v, vn, a, b in ((T.valA, "valA", 0, 12), (T.valB, "valB", 12, 16)):
+            tt(T.P1[:, 16 * a:16 * b], v[:, 16 * a:16 * b], T.cn[:, 16 * a:16 * b], A.min, vn + " cn", "P1" + vn)
+            ts(T.P2[:, a:b, 0:16], T.P1[:, 16 * a:16 * b], 0.0, A.max, "P1" + vn, "P2" + vn)
+            mm(T.hA[:, 17 * a:17 * b], T.NBO[:, :], T.P2[:, a:b, :], False, a > 0, "NBO P2pad P2" + vn, "hA")
+            if a == 0:
+                mm(T.hB[:, 0:204], T.NBO[:, :], T.P2[:, a:b, :], False, False, "NBO P2" + vn, "hB")
+                if t < 2:
+                    ts2(T.s1[:, 0:16], kT, 4.0, 1.0, A.mult, A.add, mn, "s1")
+                    cp(T.s2[:, 0:16], oT, mn, "s2")
+                    fill_val()
+                    tt(T.dum[:, :], T.s1[:, 0:16], T.s2[:, 0:16], A.subtract, "s1 s2", "dum")
+                else:
+                    fill_val()
+        if t < 2:
+            cp(T.oL[:, :], T.dum[:, :], "dum", "oL")
+            act(T.Lo[:, :], T.L[:, :].indirect(T.oL[:, :]), F.Copy, "L Lpad oL", "Lo")
+        fill_s2()
+        mm(T.hB[:, 204:272], T.NBO[:, :], T.P2[:, 12:16, :], False, True, "NBO P2valB", "hB")
+        mm(T.TP[:, 0:272], T.NBO[:, :], T.P2[:, :, :], False, False, "NBO P2valA P2valB", "TP")
+        scan(T.E[:, :], T.dE[:, :], T.hA[:, 0:272], -20000.0, A.add, A.max, "dE hA", "E")
+        cp(T.h16[:, :], T.hA[:, 0:272], "hA", "h16")
+        tt(T.eqd[:, 0:272], T.E[:, :], T.hB[:, 0:272], A.is_equal, "E hB", "edd")
+        mm(T.TP[:, 0:272], T.BO[:, :], T.eqd[:, 0:272], False, False, "BO edd", "TP")
+        o = 272
+        for q in range(15):
+            n = 17 * (15 - q)
+            ts2(T.eqd[:, o:o + n], T.h16[:, 272 - n:272], 4096.0, T.E[:, 17 * q + 16:17 * q + 17], A.add, A.is_equal, "h16 E", "ed%d" % q)
+            mm(T.TP[:, 272 - n:272], T.BO[:, :], T.eqd[:, o:o + n], False, q == 14, "BO ed%d" % q, "TP")
+            o += n
+        ts(T.hT[:, :], T.E[:, 16:272:17], 4096.0, A.subtract, "E", "hT")
+        tt(T.eqm[:, :], T.Ai[:, :].indirect(T.hT[:, :]), T.oppB[:, :], A.is_equal if t < 2 else A.not_equal, Aall + "hT oppB", "eqm")
+        if t < 2:
+            act(T.cZ[:, :], T.Z[:, :].indirect(T.hT[:, :]), F.Copy, "Z hT", "cZ")
+            mm(T.valA[:, 0:256], T.BO[:, :], T.eqm[:, :], True, True, "BO eqm", "valA")
+            act(T.xs[:, :], T.eqm[:, :], F.Identity, "eqm", "xs", -1000.0, 2000.0)
+        else:
+            act(T.cL[:, :], T.LF[:, :].indirect(T.hT[:, :]), F.Copy, "LF hT", "cL")
+        scan(T.S2[:, :], T.d17[:, :], T.TP[:, 0:272], 0.0, A.add, A.min, "d17 TP", "S2")
+        off, rn = T.rout[:, 16 * t:16 * t + 16], " rout%d " % t
+        cp(off, T.S2[:, 16:272:17], "S2", rn)
+        send(T.rin[:, 16 * t:16 * t + 16], off, "rep%d" % t, T.cores[(rank - t - 1) % N], rn)
+        if t < 2:
+            tt(T.kL[:, :], T.valA[:, 0:256], T.Lo[:, :], A.mult, "valA Lo", "kL")
+            tt(T.Z[:, :].indirect(off), T.cZ[:, :], T.kL[:, :], A.add, rn + "cZ kL", "Z")
+            op("S", lambda q: q.activation(T.DF[:, :].indirect(off), T.xs[:, :], F.Sigmoid), rn + "xs", "DF")
+            for h in range(2):
+                c = 256 * (t + 1) + 128 * h
+                act(T.DFb[:, 8 * t + 4 * h:8 * t + 4 * h + 4], T.DF[:, c:c + 128], F.Copy, "DF", "DFb%d%d" % (t, h))
+                swap(T.Pb, "Pb DFb%d%d" % (t, h), T.DFb, 8 * t, h, False, True)
+            evac(0); evac(1)
+            act(T.e4[:, :], T.eqm[:, :], F.Copy, "eqm", "e4", 0.0, 4096.0)
+            if t == 0:
+                act(T.DFb[:, 16:24], T.DF[:, 512:768], F.Copy, "DF", "DFb2")
+        else:
+            tt(T.LF[:, :].indirect(off), T.cL[:, :], T.eqm[:, :], A.mult, rn + "cL eqm", "LF")
+
+    def change(t):
+        tt(T.nA[:, :], T.Ai[:, :].indirect(T.hT[:, :]), T.e4[:, :], A.max, Aall + "hT e4", "nA")
+        cp(T.Ai[:, :].indirect(T.rout[:, 16 * t:16 * t + 16]), T.nA[:, :], "nA rout%d" % t, Aall)
+
+    def zbase(t):
+        tt(T.Z[:, rng(t)], T.zp[:, 0:8], T.Z[:, rng(t)], A.add, "zp Z", "Z")
+
+    def lf(a, b):
+        ts(T.LF[:, a:b], T.Ai[:, a:b], 4096.0, A.is_lt, Aall, "LF")
+
+    prep_tile(0)
+    ts2(T.Iz[:, :], T.dif[:, :], 0.0, 1.0 / 32, A.is_equal, A.mult, "dif", "Iz")
+    ts(T.If[:, :], T.dif[:, :], 0.0, A.is_equal, "dif", "If")
+    ts(T.offS[:, 128:256], T.offS[:, 0:128], col(2), A.add, "offS pF", "offS2")
+    cp(T.offS[:, 0:128], T.offS[:, 128:256], "offS2", "offS")
+    for k in range(4):
+        ts2(T.Pf[:, 128 * k:128 * k + 128], T.dif[:, :], 16.0 * (k // 2 - k % 2), col(3 if k // 2 else 8), A.is_equal, A.mult, "dif pF c8", "Pf%d" % k)
+    prep_pos(0)
+    for h in range(2):
+        swap(T.Pf, "Pf0 Pf1 Pf2 Pf3 Of0", T.Of4, 0, h, True, True)
+    prep_cap(0)
+    ms(T.cst[:, 0:272], 1.0 / 32, "cst")
+    ms(T.cst[:, 272:544], 3.0 / 32, "cst")
+    ms(T.cst[:, 16:544:17], -1.0 / 32, "cst")
+    ms(T.Ai[:, 2048:2320], -7, "Apad")
+    ms(T.Bi[:, 2048:2064], 2048, "Bpad")
+    consts_b()
+    gx("V", 0, 0, 2); gx("S", 0, 2, 2); zmm(0, 0)
+    gx("V", 0, 4, 1); gx("S", 0, 5, 3); zmm(0, 1)
+    evac(0); evac(1)
+    tx(0, 0); tx(0, 1)
+    prep_tile(1)
+    tx(0, 2); tx(0, 3)
+    for p in range(4):
+        gx("S", 1, 2 * p, 2)
+    offers(0, T.zp[:, 0:8], "zp")
+    iota(T.Z[:, :], [[0, 2320]], 0, 0, "Z")
+    iota(T.Wacc[:, 0:2048], [[0, 2048]], 1, 0, "Wacc")
+    iota(T.Wacc[:, 2048:2320], [[0, 272]], 0, 0, "Wacc")
+    zmm(1, 0); zmm(1, 1)
+    cp(T.colc[:, :], T.colf[:, :], "colf", "colc")
+    ts(T.NBO[:, :], T.BO[:, :], -1.0 / 4096, A.mult, "BO", "NBO")
+    for n in (256, 512):
+        act(T.W[:, n:2 * n], T.W[:, 0:n], F.Identity, "W", "W", float(n))
+    prep_tile(2)
+    prep_pos(1)
+    for h in range(2):
+        swap(T.Pf, "Of1", T.Of4, 8, h, True, False)
+    prep_cap(1); prep_cap(2)
+    tx(1, 0); tx(1, 1); tx(1, 2)
+    verdict(0, lambda: tx(1, 3), lambda: zbase(1), lambda: (consts_c(), own(0)), lambda: gx("S", 2, 0, 2))
+    offers(1, T.Z[:, 256:512], "Z")
+    gx("S", 2, 2, 2)
+    answer(0)
+    gx("S", 2, 4, 2); gx("S", 2, 6, 2)
+    prep_pos(2)
+    zmm(2, 0)
+    for h in range(2):
+        swap(T.Pf, "Of2", T.Of4, 16, h, True, False)
+        swap(T.Pb, "Pb DFb2", T.DFb, 16, h, False, False)
+    zmm(2, 1)
+    change(0)
+    tx(2, 0); tx(2, 1); tx(2, 2)
+    taken(0)
+    verdict(1, lambda: tx(2, 3), lambda: zbase(2), lambda: own(1), lambda: None)
+    offers(2, T.Z[:, 512:768], "Z")
+    change(1)
+    answer(1)
+    lf(768, 2048)
+    taken(1)
+    verdict(2, lambda: lf(0, 512), lambda: lf(512, 768), lambda: own(2), lambda: None)
+    dma("Y", "dO0", T.left[:, 768:2048], T.LF[:, 768:2048], "LF")
+    dma("S", "dO1", T.left[:, 0:512], T.LF[:, 0:512], "LF")
+    tt(T.Q2[:, :], T.LF[:, 512:768], T.Q1[:, :], A.mult, "LF Q1", "Q2")
+    said(0); said(1)
+    dma("Y", "dS0", T.said[:, 0:512], T.sd[0:128:16, 0:512], "sd0 sd1")
+    answer(2)
+    said(2)
+    dma("S", "dS1", T.said[:, 512:768], T.sd[0:128:16, 512:768], "sd2")
+
+    known = {e: {} for e in Q}
+    for o in ops:
+        o["key"] = o["sem"] or o["eng"]
+        o["clock"] = {}
+        if o["eng"] == "X":
+            continue
+        kn = known[o["eng"]]
+        for d in sorted(o["deps"], reverse=True):
+            p = ops[d]
+            if p["sem"] == "remote" or kn.get(p["key"], -1) >= d:
+                continue
+            p["need"] = True
+            o["waits"].append(d)
+            kn[p["key"]] = d
+            for a, b in p["clock"].items():
+                kn[a] = max(kn.get(a, -1), b)
+        o["clock"] = dict(kn)
+    count = {e: 0 for e in "VSPG"}
+    for o in ops:
+        if o["sem"] is None and o["need"]:
+            count[o["eng"]] += 1
+            o["cnt"] = count[o["eng"]]
+    for o in ops:
+        if o["eng"] == "X":
+            continue
+        q = Q[o["eng"]]
+        for d in o["waits"]:
+            q.wait_ge(T.sem[ops[d]["sem"] or "s" + ops[d]["eng"]], ops[d]["cnt"])
+        ins = o["fn"](q)
+        if o["sem"] is None:
+            if o["need"]:
+                ins.then_inc(T.sem["s" + o["eng"]], 1)
+        elif o["sem"] != "remote":
+            ins.then_inc(T.sem[o["sem"]], 16)
+    g.wait_ge(T.sem.sent, sent[0])
+    for s in DMAS:
+        g.sync.wait_ge(T.sem[s], 16)

@@ -7,18 +7,18 @@ def _bufs(where, dtype, spec):
 
 SCRATCH = {}
 SCRATCH.update(_bufs("sbuf", "float32", [
-    ("capF offS seg colf ZT M1 PIE K2E cn oppB Lo P1 cZ xs e4 kL Q1 Q2", [256]), ("capT ov sd", [768]), ("Z DF", [2320]),
+    ("offS seg colf ZT M1 PIE K2E cn oppB Lo P1 cZ xs e4 kL Q1 Q2", [256]), ("ov sd", [768]), ("capF capT", [64]), ("capD", [48]), ("Z DF", [2320]),
     ("W", [4104]), ("rep", [4096]), ("pF pm0 dum", [16]), ("dif If", [128]), ("Pf", [512]), ("d17 S2 dE E cTP", [272]), ("u17 s1 s2 Woh", [17]),
     ("Of4", [24, 2, 16])]))
 SCRATCH.update(_bufs("sbuf", "bfloat16", [
-    ("L", [4112]), ("LF Wacc eqd", [2320]), ("X0 X1 eq", [4096]), ("XT", [4128]), ("DFb", [24, 2, 16]), ("Iz BO b1", [128]),
-    ("Pb", [512]), ("cst", [544]), ("Fv f1", [8, 32]), ("Fj", [2048]), ("eqm cL LFo ohb accb", [256])]))
+    ("L", [4112]), ("LF Wacc eqd", [2320]), ("X0 X1 eq", [4096]), ("XT", [4128]), ("DFb", [24, 2, 16]), ("Iz b1 B32", [128]),
+    ("Pb", [512]), ("BC", [672]), ("Fv f1", [8, 32]), ("Fj", [2048]), ("eqm cL LFo ohb accb", [256])]))
 SCRATCH.update(_bufs("sbuf", "float16", [("NBO", [128]), ("h16", [272]), ("P2", [16, 17])]))
-SCRATCH.update(_bufs("sbuf", "int32", [("Ai", [2320]), ("Bi", [2064]), ("capN", [768]), ("nA", [256]), ("pI", [8]), ("k1 k2 KI iI", [16]), ("EI", [32])]))
+SCRATCH.update(_bufs("sbuf", "int32", [("Ai", [2320]), ("Bi", [2064]), ("capN", [64]), ("nA", [256]), ("pI", [8]), ("k1 k2 KI iI", [16]), ("EI", [32])]))
 SCRATCH.update(_bufs("sbuf", "uint16", [("tile", [768]), ("prm o1 iT hT oL", [16]), ("colc cand", [256]), ("msg mins", [96]), ("rin rout", [48])]))
 SCRATCH.update(_bufs("psum", "float32", [("zp pie0 pie1", [16, 2, 16]), ("valA valB hA hB TP", [512])]))
 DMAS = ["dA0", "dL", "dcap", "dcap1", "dA1", "dA2", "dB", "dO0", "dO1", "dO2", "dS0", "dS1"]
-SEMAPHORES = ["sV", "sS", "sP", "sG", "sent", "arr0", "arr1", "arr2", "rep0", "rep1", "rep2"] + DMAS
+SEMAPHORES = ["sV", "sS", "sP", "sG", "sent", "con", "arr0", "arr1", "arr2", "rep0", "rep1", "rep2"] + DMAS
 PSUM = ("zp", "pie0", "pie1", "valA", "valB", "hA", "hB", "TP")
 XS = -131072.0
 NOOFF = 127.0 * 131072.0 - 4096.0
@@ -34,8 +34,10 @@ def rank_program(g, core, T, topo):
 
     def op(eng, fn, r="", w="", sem=None, cnt=0):
         r, w = r.split(), w.split()
-        w += [x for x in r if x in PSUM]
         deps = set(lastw[x] for x in r + w if x in lastw)
+        for x in r:
+            if x in PSUM:
+                deps.update(d for d in readers.get(x, ()) if ops[d]["eng"] != eng)
         for x in w:
             deps.update(readers.get(x, ()))
         if eng == "P":
@@ -58,7 +60,9 @@ def rank_program(g, core, T, topo):
     def act(out, a, f, r, w, bias=0.0, scale=1.0): op("S", lambda q: q.activation(out, a, f, bias=bias, scale=scale), r, w)
     def mm(out, l, rhs, st, sp, r, w): op("P", lambda q: q.matmul(out, l, rhs, st, sp), r, w)
     def iota(out, pat, base, cm, w): op("G", lambda q: q.iota(out, pat, base, cm, allow_small_or_imprecise_dtypes=True), "", w)
+    def ioti(out, pat, base, cm, w): op("G", lambda q: q.iota(out, pat, base, cm), "", w)
     def sel(out, a, pat, cmp, fill, base, cm, r, w): op("G", lambda q: q.affine_select(out, a, pat, cmp, fill, base, cm), r, w)
+    def gcp(out, a, n, r, w): sel(out, a, [[0, n]], A.is_ge, 0.0, 0, 0, r, w)
 
     sent = [0]
 
@@ -73,6 +77,7 @@ def rank_program(g, core, T, topo):
 
     Xb, Xn = [T.X0, T.X1, T.X0], ["X0", "X1", "X0"]
     pie = [T.pie0, T.pie1]
+    BO, c1, c3 = T.BC[:, 0:128], T.BC[:, 128:400], T.BC[:, 400:672]
     Aall = " A0 A1 A2 Apad "
     def col(j): return T.pF[:, j:j + 1]
     def rng(t): return slice(256 * t, 256 * t + 256)
@@ -80,44 +85,51 @@ def rank_program(g, core, T, topo):
     def Xu(t, u, n): return " " + " ".join("%s_%d" % (Xn[t], k) for k in range(u, u + n))
 
     dma("Y", "dA0", T.Ai[:, 0:256], T.acct[:, 0:256], "", "A0")
-    ms(T.capN[:, 0:256], 0, "capN0")
-    dma("Y", "dcap", T.capN[0:128:16, 0:256], T.cap[:, 0:256], "", "capN0")
+    dma("S", "dcap", T.capN[:, 0:32], T.cap[:, 0:512], "", "capN0")
+    dma("S", "dcap1", T.capN[:, 32:64], T.cap[:, 256:768], "", "capN1")
     dma("Y", "dL", T.L[:, 0:4096], T.loss[:, :], "", "L")
-    ms(T.capN[:, 256:768], 0, "capN1")
     dma("Y", "dA1", T.Ai[:, 256:768], T.acct[:, 256:768], "L", "A1")
-    dma("Y", "dcap1", T.capN[0:128:16, 256:768], T.cap[:, 256:768], "", "capN1")
     dma("Y", "dB", T.Bi[:, 0:2048], T.book[:, :], "", "B")
     dma("Y", "dA2", T.Ai[:, 768:2048], T.acct[:, 768:2048], "", "A2")
 
-    op("G", lambda q: q.iota(T.pI[:, 0:1], [[0, 1]], 0, 1), "", "pI0")
+    iota(T.W[:, 0:256], [[2, 128], [-1, 2]], 1, 0, "W")
+    ioti(T.pI[:, 0:1], [[0, 1]], 0, 1, "pI0")
     iota(T.pm0[:, :], [[32, 8], [8, 2]], 0, 0, "pm0")
     iota(T.dif[:, :], [[-1, 128]], 0, 1, "dif")
     iota(T.offS[:, 0:128], [[512, 4], [0, 2], [32, 16]], 0, 0, "offS")
-    iota(T.f1[:, :, :], [[0, 256]], -131072, 0, "f1")
-    sel(T.Fv[:, :, :], T.f1[:, :, :], [[0, 8], [1, 32]], A.is_gt, 0.0, -15, 0, "f1", "Fv")
-    sel(T.Fv[:, :, :], T.Fv[:, :, :], [[0, 8], [1, 32]], A.not_equal, 4096.0, -15, 0, "Fv", "Fv")
-    sel(T.Fv[:, :, :], T.Fv[:, :, :], [[-16, 8], [0, 32]], A.is_ge, 0.0, 0, 1, "Fv", "Fv")
-    sel(T.Fv[:, :, :], T.Fv[:, :, :], [[16, 8], [0, 32]], A.is_ge, 0.0, 15, -1, "Fv", "Fv")
     iota(T.u17[:, :], [[1, 17]], 0, 0, "u17")
     iota(T.dum[:, :], [[16, 16]], 2049, 0, "dum")
     iota(T.colf[:, :], [[1, 256]], 0, 0, "colf")
-    iota(T.b1[:, :], [[0, 128]], 4096, 0, "b1")
-    sel(T.BO[:, :], T.b1[:, :], [[-16, 8], [0, 16]], A.is_ge, 0.0, 0, 1, "b1", "BO")
-    sel(T.BO[:, :], T.BO[:, :], [[16, 8], [0, 16]], A.is_ge, 0.0, 15, -1, "BO", "BO")
-    iota(T.W[:, 0:256], [[2, 128], [-1, 2]], 1, 0, "W")
-    iota(T.W[:, 1024:4104], [[2, 1540], [-1, 2]], 1025, 0, "W1")
-
+    iota(T.cTP[:, :], [[0, 272]], 2048, 0, "cTP")
+    other = T.cores[rank ^ 1]
+    if rank % 2 == 0:
+        iota(T.f1[:, :, :], [[0, 256]], -131072, 0, "f1")
+        sel(T.Fv[:, :, :], T.f1[:, :, :], [[0, 8], [1, 32]], A.is_gt, 0.0, -15, 0, "f1", "Fv")
+        sel(T.Fv[:, :, :], T.Fv[:, :, :], [[0, 8], [1, 32]], A.not_equal, 4096.0, -15, 0, "Fv", "Fv")
+        sel(T.Fv[:, :, :], T.Fv[:, :, :], [[-16, 8], [0, 32]], A.is_ge, 0.0, 0, 1, "Fv", "Fv")
+        sel(T.Fv[:, :, :], T.Fv[:, :, :], [[16, 8], [0, 32]], A.is_ge, 0.0, 15, -1, "Fv", "Fv")
+        send(T.Fv[:, :, :], T.Fv[:, :, :], "con", other, "Fv")
+        arrive("BO cst", "con", other)
+    else:
+        iota(T.b1[:, :], [[0, 128]], 4096, 0, "b1")
+        sel(BO, T.b1[:, :], [[-16, 8], [0, 16]], A.is_ge, 0.0, 0, 1, "b1", "BO")
+        sel(BO, BO, [[16, 8], [0, 16]], A.is_ge, 0.0, 15, -1, "BO", "BO")
+        iota(c1, [[0, 272]], 1, 0, "cst")
+        iota(c3, [[0, 272]], 3, 0, "cst")
+        iota(T.BC[:, 144:672:17], [[0, 32]], -1, 0, "cst")
+        send(T.BC[:, :], T.BC[:, :], "con", other, "BO cst")
+        arrive("Fv", "con", other)
+    iota(T.Z[:, 0:1024], [[0, 1024]], 0, 0, "Z")
+    ioti(T.Ai[:, 2048:2320], [[0, 272]], -7, 0, "Apad")
+    ioti(T.Bi[:, 2048:2064], [[0, 16]], 2048, 0, "Bpad")
+    for n in (256, 512, 1024, 2048):
+        act(T.W[:, n:2 * n], T.W[:, 0:n], F.Identity, "W", "W", float(n))
+    act(T.W[:, 4096:4104], T.W[:, 0:8], F.Identity, "W", "W", 4096.0)
     ms(T.seg[:, :], 0.0, "seg")
     ms(T.seg[:, 0:256:16], 2.0 ** 27, "seg")
-    ms(T.LF[:, 2048:2320], 0.0, "LF")
     ms(T.L[:, 4096:4112], 0.0, "Lpad")
     ms(T.XT[:, 2048:2064], 0.0, "XTpad0")
     ms(T.XT[:, 4112:4128], 0.0, "XTpad1")
-    for j in (1, 2):
-        act(T.DF[:, rng(j)], T.seg[:, :], F.Sigmoid, "seg", "DF", -1000.0, 0.0)
-    for j in range(16):
-        act(T.Fj[:, 128 * j:128 * j + 128], T.Fv[:, :, 15 - j:31 - j], F.Copy, "Fv", "Fj%d" % j)
-    lastw["Fj"] = lastw["Fj15"]
     p0 = T.pI[:, 0:1]
     ts(T.pI[:, 1:2], p0, 15, A.bitwise_and, "pI0", "pI1")
     ts(T.pI[:, 2:3], p0, 31, A.bitwise_and, "pI0", "pI2")
@@ -136,9 +148,13 @@ def rank_program(g, core, T, topo):
     def prep_pos(t):
         cp(T.Of4[:, 8 * t:8 * t + 8], T.Ai[:, rng(t)], An(t), "Of%d" % t)
 
-    def prep_cap(t):
-        ts2(T.capF[:, :], T.capN[:, rng(t)], -4096.0, -2048.0, A.mult, A.add, "capN%d" % min(t, 1), "capF")
-        tr(T.capT[:, rng(t)], T.capF[:, :], "capF", "capT%d" % t)
+    def prep_cap():
+        ts2(T.capF[:, :], T.capN[:, :], -4096.0, -2048.0, A.mult, A.add, "capN0 capN1", "capF")
+        tr(T.capT[:, :], T.capF[:, :], "capF", "capT")
+        for t in range(3):
+            for gl in range(2):
+                c = 16 * gl + (0, 8, 40)[t]
+                cp(T.capD[:, 16 * t + gl:16 * t + 16:2], T.capT[:, c:c + 8], "capT", "capD%d%d" % (t, gl))
 
     def swap(l, r, rhs4, b0, h, st, sp):
         for k in range(4):
@@ -161,8 +177,15 @@ def rank_program(g, core, T, topo):
     def zmm(t, h):
         if h == 0:
             mm(T.zp[:, 0:8], T.If[:, :], T.offS[:, :], True, False, "If offS", "zp")
+        if h == 0 and t == 2:
+            mm(T.zp[:, 0:8], T.If[:, :], T.Z[:, rng(2)], False, False, "If Z", "zp")
         for k in range(32):
             mm(T.zp[:, 4 * h:4 * h + 4, k // 16, :], T.Iz[:, :], Xb[t][:, 2048 * h + k:2048 * h + 2048:32], False, h == 1 and k == 31, "Iz" + Xu(t, 4 * h, 4), "zp")
+
+    def marks():
+        for j in (1, 2):
+            act(T.DF[:, rng(j)], T.seg[:, :], F.Sigmoid, "seg", "DF", -1000.0, 0.0)
+        act(T.Pb[:, :], T.Pf[:, :], F.Copy, "Pf0 Pf1 Pf2 Pf3", "Pb", 0.0, 2.0 ** 26)
 
     def consts_b():
         ts(T.Woh[:, :], T.u17[:, :], col(1), A.is_equal, "u17 pF", "Woh")
@@ -173,20 +196,13 @@ def rank_program(g, core, T, topo):
         tt(T.dE[:, 17:34], T.s1[:, :], T.s2[:, :], A.add, "s1 s2", "dE1")
         ts(T.d17[:, 0:16], T.d17[:, 17:33], 2.0 ** 22, A.mult, "d17a d17b", "d17 d17b")
         ts(T.dE[:, 0:17], T.dE[:, 17:34], 4096.0, A.mult, "dE1", "dE dE1")
-        ms(T.cTP[:, :], 2048.0, "cTP")
         ms(T.P2[:, :, 16], 0.0, "P2pad")
         ts(T.cTP[:, 16:272:17], T.dum[:, :], col(1), A.add, "dum pF", "cTP")
-
-    def consts_c():
-        for n in (1, 2, 4, 8):
-            act(T.dE[:, 17 * n:34 * n], T.dE[:, 0:17 * n], F.Copy, "dE", "dE")
-            act(T.d17[:, 17 * n:34 * n], T.d17[:, 0:17 * n], F.Copy, "d17", "d17")
-        act(T.Pb[:, :], T.Pf[:, :], F.Copy, "Pf0 Pf1 Pf2 Pf3", "Pb", 0.0, 2.0 ** 26)
 
     def offers(t, src, sn):
         tr(T.ZT[:, :], src, sn, "ZT")
         scan(T.M1[:, :], T.seg[:, :], T.ZT[:, :], 0.0, A.add, A.min, "seg ZT", "M1")
-        tt(T.k1[:, :], T.M1[:, 15:256:16], T.capT[:, 256 * t:256 * t + 256:16], A.min, "M1 capT%d" % t, "k1")
+        tt(T.k1[:, :], T.M1[:, 15:256:16], T.capD[:, 16 * t:16 * t + 16], A.min, "M1 capD%d0 capD%d1" % (t, t), "k1")
         ts(T.k2[:, :], T.k1[:, :], 4095, A.bitwise_and, "k1", "k2")
         cp(T.o1[:, :], T.k2[:, :], "k2", "o1")
         for h in range(2):
@@ -206,7 +222,9 @@ def rank_program(g, core, T, topo):
     def own(t):
         if t < 2: act(T.ohb[:, :], T.Woh[:, 0:16].indirect(T.iT[:, :]), F.Identity, "Woh iT", "ohb", XS, -XS)
         else: act(T.Q1[:, :], T.Woh[:, 0:16].indirect(T.iT[:, :]), F.Identity, "Woh iT", "Q1", 2.0, -1.0)
-        act(T.ov[:, rng(t)], T.W[:, :].indirect(T.msg[:, 32 * t:32 * t + 16]), F.Sign, "W W1 msg%d" % t, "ov%d" % t, 4097.0, -1.0)
+
+    def over(t):
+        act(T.ov[:, rng(t)], T.W[:, :].indirect(T.msg[:, 32 * t:32 * t + 16]), F.Sign, "W msg%d" % t, "ov%d" % t, 4097.0, -1.0)
 
     def acc(t): return T.Wacc[:, :].indirect(T.rin[:, 16 * t:16 * t + 16])
 
@@ -227,14 +245,14 @@ def rank_program(g, core, T, topo):
         tt(T.sd[:, rng(t)], acc(t), T.ov[:, rng(t)], A.add, "Wacc rin%d ov%d" % (t, t), "sd%d" % t)
 
     def verdict(t, fill_rep, fill_val, fill_s, fill_s2):
-        mm(T.hA[:, 0:272], T.BO[:, :], T.cst[:, 0:272], True, False, "BO cst", "hA")
-        mm(T.hB[:, 0:272], T.BO[:, :], T.cst[:, 272:544], True, False, "BO cst", "hB")
+        mm(T.hA[:, 0:272], T.B32[:, :], c1, True, False, "B32 cst", "hA")
+        mm(T.hB[:, 0:272], T.B32[:, :], c3, True, False, "B32 cst", "hB")
         mm(T.TP[:, 0:272], T.If[:, :], T.cTP[:, :], True, False, "If cTP", "TP")
         mn = " min%d " % t
         arrive(mn, "arr%d" % t, T.cores[(rank - t - 1) % N])
         oT, kT = T.mins[:, 32 * t:32 * t + 16], T.mins[:, 32 * t + 16:32 * t + 32]
         cp(T.cand[:, :], T.Bi[:, :].indirect(kT), "B Bpad" + mn, "cand")
-        act(T.oppB[:, :], T.W[:, :].indirect(oT), F.Copy, "W W1" + mn, "oppB")
+        act(T.oppB[:, :], T.W[:, :].indirect(oT), F.Copy, "W" + mn, "oppB")
         ts2(T.cn[:, :], T.cand[:, :], -1.0, 2048.0, A.mult, A.add, "cand", "cn")
         fill_rep()
         for k in range(8):
@@ -245,7 +263,7 @@ def rank_program(g, core, T, topo):
                 b = k // 2
                 for j in range(16):
                     mm((T.valB if b == 3 else T.valA)[:, 64 * b:64 * b + 64], T.Fj[:, 128 * j:128 * j + 128], T.eq[:, 1024 * b + j:1024 * b + 1024:16],
-                       j == 0, j == 15, "Fj eq%d eq%d" % (k - 1, k), "valB" if b == 3 else "valA")
+                       j == 0, j == 15, "Fj%d eq%d eq%d" % (j, k - 1, k), "valB" if b == 3 else "valA")
         fill_s()
         for v, vn, a, b in ((T.valA, "valA", 0, 12), (T.valB, "valB", 12, 16)):
             tt(T.P1[:, 16 * a:16 * b], v[:, 16 * a:16 * b], T.cn[:, 16 * a:16 * b], A.min, vn + " cn", "P1" + vn)
@@ -256,10 +274,8 @@ def rank_program(g, core, T, topo):
                 if t < 2:
                     ts2(T.s1[:, 0:16], kT, 4.0, 1.0, A.mult, A.add, mn, "s1")
                     cp(T.s2[:, 0:16], oT, mn, "s2")
-                    fill_val()
                     tt(T.dum[:, :], T.s1[:, 0:16], T.s2[:, 0:16], A.subtract, "s1 s2", "dum")
-                else:
-                    fill_val()
+                fill_val()
         if t < 2:
             cp(T.oL[:, :], T.dum[:, :], "dum", "oL")
             act(T.Lo[:, :], T.L[:, :].indirect(T.oL[:, :]), F.Copy, "L Lpad oL", "Lo")
@@ -269,18 +285,18 @@ def rank_program(g, core, T, topo):
         scan(T.E[:, :], T.dE[:, :], T.hA[:, 0:272], -20000.0, A.add, A.max, "dE hA", "E")
         cp(T.h16[:, :], T.hA[:, 0:272], "hA", "h16")
         tt(T.eqd[:, 0:272], T.E[:, :], T.hB[:, 0:272], A.is_equal, "E hB", "edd")
-        mm(T.TP[:, 0:272], T.BO[:, :], T.eqd[:, 0:272], False, False, "BO edd", "TP")
+        mm(T.TP[:, 0:272], BO, T.eqd[:, 0:272], False, False, "BO edd", "TP")
         o = 272
         for q in range(15):
             n = 17 * (15 - q)
             ts2(T.eqd[:, o:o + n], T.h16[:, 272 - n:272], 4096.0, T.E[:, 17 * q + 16:17 * q + 17], A.add, A.is_equal, "h16 E", "ed%d" % q)
-            mm(T.TP[:, 272 - n:272], T.BO[:, :], T.eqd[:, o:o + n], False, q == 14, "BO ed%d" % q, "TP")
+            mm(T.TP[:, 272 - n:272], BO, T.eqd[:, o:o + n], False, q == 14, "BO ed%d" % q, "TP")
             o += n
         ts(T.hT[:, :], T.E[:, 16:272:17], 4096.0, A.subtract, "E", "hT")
         tt(T.eqm[:, :], T.Ai[:, :].indirect(T.hT[:, :]), T.oppB[:, :], A.is_equal if t < 2 else A.not_equal, Aall + "hT oppB", "eqm")
         if t < 2:
             act(T.cZ[:, :], T.Z[:, :].indirect(T.hT[:, :]), F.Copy, "Z hT", "cZ")
-            mm(T.valA[:, 0:256], T.BO[:, :], T.eqm[:, :], True, True, "BO eqm", "valA")
+            mm(T.valA[:, 0:256], BO, T.eqm[:, :], True, True, "BO eqm", "valA")
             act(T.xs[:, :], T.eqm[:, :], F.Identity, "eqm", "xs", -1000.0, 2000.0)
         else:
             act(T.cL[:, :], T.LF[:, :].indirect(T.hT[:, :]), F.Copy, "LF hT", "cL")
@@ -308,7 +324,7 @@ def rank_program(g, core, T, topo):
         cp(T.Ai[:, :].indirect(T.rout[:, 16 * t:16 * t + 16]), T.nA[:, :], "nA rout%d" % t, Aall)
 
     def zbase(t):
-        tt(T.Z[:, rng(t)], T.zp[:, 0:8], T.Z[:, rng(t)], A.add, "zp Z", "Z")
+        act(T.Z[:, rng(t)], T.zp[:, 0:8], F.Copy, "zp", "Z")
 
     def lf(a, b):
         ts(T.LF[:, a:b], T.Ai[:, a:b], 4096.0, A.is_lt, Aall, "LF")
@@ -323,39 +339,41 @@ def rank_program(g, core, T, topo):
     prep_pos(0)
     for h in range(2):
         swap(T.Pf, "Pf0 Pf1 Pf2 Pf3 Of0", T.Of4, 0, h, True, True)
-    prep_cap(0)
-    ms(T.cst[:, 0:272], 1.0 / 32, "cst")
-    ms(T.cst[:, 272:544], 3.0 / 32, "cst")
-    ms(T.cst[:, 16:544:17], -1.0 / 32, "cst")
-    ms(T.Ai[:, 2048:2320], -7, "Apad")
-    ms(T.Bi[:, 2048:2064], 2048, "Bpad")
-    consts_b()
+    prep_cap()
+    cp(T.colc[:, :], T.colf[:, :], "colf", "colc")
     gx("V", 0, 0, 2); gx("S", 0, 2, 2); zmm(0, 0)
     gx("V", 0, 4, 1); gx("S", 0, 5, 3); zmm(0, 1)
     evac(0); evac(1)
     tx(0, 0); tx(0, 1)
     prep_tile(1)
+    consts_b()
     tx(0, 2); tx(0, 3)
     for p in range(4):
         gx("S", 1, 2 * p, 2)
     offers(0, T.zp[:, 0:8], "zp")
-    iota(T.Z[:, :], [[0, 2320]], 0, 0, "Z")
+    for j in range(12, 16):
+        gcp(T.Fj[:, 128 * j:128 * j + 128], T.Fv[:, :, 15 - j:31 - j], 128, "Fv", "Fj%d" % j)
+    for n in (1, 2, 4, 8):
+        gcp(T.dE[:, 17 * n:34 * n], T.dE[:, 0:17 * n], 17 * n, "dE", "dE")
+        gcp(T.d17[:, 17 * n:34 * n], T.d17[:, 0:17 * n], 17 * n, "d17", "d17")
+    iota(T.LF[:, 2048:2320], [[0, 272]], 0, 0, "LF")
+    iota(T.Z[:, 1024:2320], [[0, 1296]], 0, 0, "Z")
     iota(T.Wacc[:, 0:2048], [[0, 2048]], 1, 0, "Wacc")
-    iota(T.Wacc[:, 2048:2320], [[0, 272]], 0, 0, "Wacc")
+    iota(T.Wacc[:, 2048:2320], [[0, 272]], 0, 0, "Wacc1")
+    lastw["Wacc"] = lastw["Wacc1"]
     zmm(1, 0); zmm(1, 1)
-    cp(T.colc[:, :], T.colf[:, :], "colf", "colc")
-    ts(T.NBO[:, :], T.BO[:, :], -1.0 / 4096, A.mult, "BO", "NBO")
-    for n in (256, 512):
-        act(T.W[:, n:2 * n], T.W[:, 0:n], F.Identity, "W", "W", float(n))
+    ts(T.NBO[:, :], BO, -1.0 / 4096, A.mult, "BO", "NBO")
+    for j in range(12):
+        cp(T.Fj[:, 128 * j:128 * j + 128], T.Fv[:, :, 15 - j:31 - j], "Fv", "Fj%d" % j)
+    ts(T.B32[:, :], BO, 1.0 / 32, A.mult, "BO", "B32")
     prep_tile(2)
     prep_pos(1)
     for h in range(2):
         swap(T.Pf, "Of1", T.Of4, 8, h, True, False)
-    prep_cap(1); prep_cap(2)
     tx(1, 0); tx(1, 1); tx(1, 2)
-    verdict(0, lambda: tx(1, 3), lambda: zbase(1), lambda: (consts_c(), own(0)), lambda: gx("S", 2, 0, 2))
+    verdict(0, lambda: tx(1, 3), lambda: None, lambda: (marks(), zbase(1), own(0), gx("S", 2, 0, 2)), lambda: gx("S", 2, 2, 1))
     offers(1, T.Z[:, 256:512], "Z")
-    gx("S", 2, 2, 2)
+    gx("S", 2, 3, 1)
     answer(0)
     gx("S", 2, 4, 2); gx("S", 2, 6, 2)
     prep_pos(2)
@@ -367,13 +385,13 @@ def rank_program(g, core, T, topo):
     change(0)
     tx(2, 0); tx(2, 1); tx(2, 2)
     taken(0)
-    verdict(1, lambda: tx(2, 3), lambda: zbase(2), lambda: own(1), lambda: None)
+    verdict(1, lambda: tx(2, 3), lambda: None, lambda: (zbase(2), own(1)), lambda: None)
     offers(2, T.Z[:, 512:768], "Z")
     change(1)
     answer(1)
     lf(768, 2048)
     taken(1)
-    verdict(2, lambda: lf(0, 512), lambda: lf(512, 768), lambda: own(2), lambda: None)
+    verdict(2, lambda: lf(0, 512), lambda: lf(512, 768), lambda: (own(2), over(0), over(1), over(2)), lambda: None)
     dma("Y", "dO0", T.left[:, 768:2048], T.LF[:, 768:2048], "LF")
     dma("S", "dO1", T.left[:, 0:512], T.LF[:, 0:512], "LF")
     tt(T.Q2[:, :], T.LF[:, 512:768], T.Q1[:, :], A.mult, "LF Q1", "Q2")

from concourse.mybir import AluOpType as A, ActivationFunctionType as F


def _bufs(where, dtype, spec):
    return {n: (where, [128] + list(sh), dtype) for names, sh in spec for n in names.split()}


SCRATCH = {}
SCRATCH.update(_bufs("sbuf", "float32", [
    ("offS seg colf ZT M1 PIE K2E cn oppB Lo P1 cZ xs e4 kL Q1 Q2", [256]), ("ov sd", [768]), ("capF capT", [64]), ("capD", [48]), ("Z DF", [2320]),
    ("W", [4104]), ("rep", [4096]), ("pF pm0 dum", [16]), ("dif If", [128]), ("Pf", [512]), ("d17 S2 dE E cTP", [272]), ("u17 s1 s2 Woh", [17]),
    ("Of4", [24, 2, 16])]))
SCRATCH.update(_bufs("sbuf", "bfloat16", [
    ("L", [4112]), ("LF Wacc eqd", [2320]), ("X0 X1 eq", [4096]), ("XT", [4128]), ("DFb", [24, 2, 16]), ("Iz b1 B32", [128]),
    ("Pb", [512]), ("BC", [672]), ("Fv f1", [8, 32]), ("Fj", [2048]), ("eqm cL LFo ohb accb", [256])]))
SCRATCH.update(_bufs("sbuf", "float16", [("NBO", [128]), ("h16", [272]), ("P2", [16, 17])]))
SCRATCH.update(_bufs("sbuf", "int32", [("Ai", [2320]), ("Bi", [2064]), ("capN", [64]), ("nA", [256]), ("pI", [8]), ("k1 k2 KI iI", [16]), ("EI", [32])]))
SCRATCH.update(_bufs("sbuf", "uint16", [("tile", [768]), ("prm o1 iT hT oL", [16]), ("colc cand", [256]), ("msg mins", [96]), ("rin rout", [48])]))
SCRATCH.update(_bufs("psum", "float32", [("zp pie0 pie1", [16, 2, 16]), ("valA valB hA hB TP", [512])]))
DMAS = ["dA0", "dL", "dcap", "dcap1", "dA1", "dA2", "dB", "dO0", "dO1", "dO2", "dS0", "dS1"]
SEMAPHORES = ["sV", "sS", "sP", "sG", "sent", "con", "arr0", "arr1", "arr2", "rep0", "rep1", "rep2"] + DMAS
PSUM = ("zp", "pie0", "pie1", "valA", "valB", "hA", "hB", "TP")
XS = -131072.0
NOOFF = 127.0 * 131072.0 - 4096.0


def rank_program(g, core, T, topo):
    rank = T.rank_of(core)
    if rank is None:
        return
    N = len(T.cores)
    Q = {"V": g.vector, "S": g.scalar, "P": g.tensor, "G": g, "Y": g.sync}
    ops, lastw, readers = [], {}, {}

    def op(eng, fn, r="", w="", sem=None, cnt=0):
        r, w = r.split(), w.split()
        deps = set(lastw[x] for x in r + w if x in lastw)
        for x in r:
            if x in PSUM:
                deps.update(d for d in readers.get(x, ()) if ops[d]["eng"] != eng)
        for x in w:
            deps.update(readers.get(x, ()))
        if eng == "P":
            deps = set(d for d in deps if ops[d]["eng"] != "P")
        ops.append({"eng": eng, "fn": fn, "deps": deps, "sem": sem, "cnt": cnt, "need": False, "waits": []})
        for x in r:
            readers.setdefault(x, []).append(len(ops) - 1)
        for x in w:
            lastw[x] = len(ops) - 1
            readers[x] = []

    def dma(eng, sem, out, in_, r="", w=""): op(eng, lambda q: q.dma_start(out, in_), r, w, sem, 16)
    def ts(out, a, x, o0, r, w): op("V", lambda q: q.tensor_scalar(out, a, x, None, o0), r, w)
    def ts2(out, a, x, y, o0, o1, r, w): op("V", lambda q: q.tensor_scalar(out, a, x, y, o0, o1), r, w)
    def tt(out, a, b, o, r, w): op("V", lambda q: q.tensor_tensor(out, a, b, o), r, w)
    def cp(out, a, r, w): op("V", lambda q: q.tensor_copy(out, a), r, w)
    def tr(out, a, r, w): op("V", lambda q: q.transpose(out, a), r, w)
    def ms(out, c, w): op("V", lambda q: q.memset(out, c), "", w)
    def scan(out, d0, d1, init, o0, o1, r, w): op("V", lambda q: q.tensor_tensor_scan(out, d0, d1, init, o0, o1), r, w)
    def act(out, a, f, r, w, bias=0.0, scale=1.0): op("S", lambda q: q.activation(out, a, f, bias=bias, scale=scale), r, w)
    def mm(out, l, rhs, st, sp, r, w): op("P", lambda q: q.matmul(out, l, rhs, st, sp), r, w)
    def iota(out, pat, base, cm, w): op("G", lambda q: q.iota(out, pat, base, cm, allow_small_or_imprecise_dtypes=True), "", w)
    def ioti(out, pat, base, cm, w): op("G", lambda q: q.iota(out, pat, base, cm), "", w)
    def sel(out, a, pat, cmp, fill, base, cm, r, w): op("G", lambda q: q.affine_select(out, a, pat, cmp, fill, base, cm), r, w)
    def gcp(out, a, n, r, w): sel(out, a, [[0, n]], A.is_ge, 0.0, 0, 0, r, w)

    sent = [0]

    def send(out, in_, sem, peer, r):
        rid, pid, _ = topo.addr(peer)
        es = topo.engines(core, peer)[:8]
        sent[0] += len(es)
        op("G", lambda q: q.remote_dma(out, in_, T.sem[sem], T.sem.sent, pid, rid, sum(1 << e for e in es)), r, "", "remote")

    def arrive(name, sem, peer):
        op("X", None, "", name, sem, len(topo.engines(peer, core)[:8]))

    Xb, Xn = [T.X0, T.X1, T.X0], ["X0", "X1", "X0"]
    pie = [T.pie0, T.pie1]
    BO, c1, c3 = T.BC[:, 0:128], T.BC[:, 128:400], T.BC[:, 400:672]
    Aall = " A0 A1 A2 Apad "
    def col(j): return T.pF[:, j:j + 1]
    def rng(t): return slice(256 * t, 256 * t + 256)
    def An(t): return " A%d " % min(t, 1)
    def Xu(t, u, n): return " " + " ".join("%s_%d" % (Xn[t], k) for k in range(u, u + n))

    dma("Y", "dA0", T.Ai[:, 0:256], T.acct[:, 0:256], "", "A0")
    dma("S", "dcap", T.capN[:, 0:32], T.cap[:, 0:512], "", "capN0")
    dma("S", "dcap1", T.capN[:, 32:64], T.cap[:, 256:768], "", "capN1")
    dma("Y", "dL", T.L[:, 0:4096], T.loss[:, :], "", "L")
    dma("Y", "dA1", T.Ai[:, 256:768], T.acct[:, 256:768], "L", "A1")
    dma("Y", "dB", T.Bi[:, 0:2048], T.book[:, :], "", "B")
    dma("Y", "dA2", T.Ai[:, 768:2048], T.acct[:, 768:2048], "", "A2")

    iota(T.W[:, 0:256], [[2, 128], [-1, 2]], 1, 0, "W")
    ioti(T.pI[:, 0:1], [[0, 1]], 0, 1, "pI0")
    iota(T.pm0[:, :], [[32, 8], [8, 2]], 0, 0, "pm0")
    iota(T.dif[:, :], [[-1, 128]], 0, 1, "dif")
    iota(T.offS[:, 0:128], [[512, 4], [0, 2], [32, 16]], 0, 0, "offS")
    iota(T.u17[:, :], [[1, 17]], 0, 0, "u17")
    iota(T.dum[:, :], [[16, 16]], 2049, 0, "dum")
    iota(T.colf[:, :], [[1, 256]], 0, 0, "colf")
    iota(T.cTP[:, :], [[0, 272]], 2048, 0, "cTP")
    other = T.cores[rank ^ 1]
    if rank % 2 == 0:
        iota(T.f1[:, :, :], [[0, 256]], -131072, 0, "f1")
        sel(T.Fv[:, :, :], T.f1[:, :, :], [[0, 8], [1, 32]], A.is_gt, 0.0, -15, 0, "f1", "Fv")
        sel(T.Fv[:, :, :], T.Fv[:, :, :], [[0, 8], [1, 32]], A.not_equal, 4096.0, -15, 0, "Fv", "Fv")
        sel(T.Fv[:, :, :], T.Fv[:, :, :], [[-16, 8], [0, 32]], A.is_ge, 0.0, 0, 1, "Fv", "Fv")
        sel(T.Fv[:, :, :], T.Fv[:, :, :], [[16, 8], [0, 32]], A.is_ge, 0.0, 15, -1, "Fv", "Fv")
        send(T.Fv[:, :, :], T.Fv[:, :, :], "con", other, "Fv")
        arrive("BO cst", "con", other)
    else:
        iota(T.b1[:, :], [[0, 128]], 4096, 0, "b1")
        sel(BO, T.b1[:, :], [[-16, 8], [0, 16]], A.is_ge, 0.0, 0, 1, "b1", "BO")
        sel(BO, BO, [[16, 8], [0, 16]], A.is_ge, 0.0, 15, -1, "BO", "BO")
        iota(c1, [[0, 272]], 1, 0, "cst")
        iota(c3, [[0, 272]], 3, 0, "cst")
        iota(T.BC[:, 144:672:17], [[0, 32]], -1, 0, "cst")
        send(T.BC[:, :], T.BC[:, :], "con", other, "BO cst")
        arrive("Fv", "con", other)
    iota(T.Z[:, 0:1024], [[0, 1024]], 0, 0, "Z")
    ioti(T.Ai[:, 2048:2320], [[0, 272]], -7, 0, "Apad")
    ioti(T.Bi[:, 2048:2064], [[0, 16]], 2048, 0, "Bpad")
    for n in (256, 512, 1024, 2048):
        act(T.W[:, n:2 * n], T.W[:, 0:n], F.Identity, "W", "W", float(n))
    act(T.W[:, 4096:4104], T.W[:, 0:8], F.Identity, "W", "W", 4096.0)
    ms(T.seg[:, :], 0.0, "seg")
    ms(T.seg[:, 0:256:16], 2.0 ** 27, "seg")
    ms(T.L[:, 4096:4112], 0.0, "Lpad")
    ms(T.XT[:, 2048:2064], 0.0, "XTpad0")
    ms(T.XT[:, 4112:4128], 0.0, "XTpad1")
    p0 = T.pI[:, 0:1]
    ts(T.pI[:, 1:2], p0, 15, A.bitwise_and, "pI0", "pI1")
    ts(T.pI[:, 2:3], p0, 31, A.bitwise_and, "pI0", "pI2")
    ts2(T.pI[:, 3:4], p0, 4, 1, A.arith_shift_right, A.bitwise_and, "pI0", "pI3")
    ts(T.pI[:, 4:5], p0, 1, A.bitwise_and, "pI0", "pI4")
    ts2(T.pI[:, 5:6], p0, 1, 7, A.arith_shift_right, A.bitwise_and, "pI0", "pI5")
    cp(T.pF[:, 0:6], T.pI[:, 0:6], "pI0 pI1 pI2 pI3 pI4 pI5", "pF")
    ts2(col(7), col(4), 16.0, col(5), A.mult, A.add, "pF", "c7")
    ts2(col(8), col(3), -1.0, 1.0, A.mult, A.add, "pF", "c8")
    ts2(col(9), col(1), 8192.0, 127.0 * 131072.0, A.mult, A.add, "pF", "c9")
    ts(T.prm[:, :], T.pm0[:, :], col(7), A.add, "pm0 c7", "prm")

    def prep_tile(t):
        cp(T.tile[:, rng(t)], T.Ai[:, rng(t)].indirect(T.prm[:, :]), An(t) + "prm", "tile%d" % t)

    def prep_pos(t):
        cp(T.Of4[:, 8 * t:8 * t + 8], T.Ai[:, rng(t)], An(t), "Of%d" % t)

    def prep_cap():
        ts2(T.capF[:, :], T.capN[:, :], -4096.0, -2048.0, A.mult, A.add, "capN0 capN1", "capF")
        tr(T.capT[:, :], T.capF[:, :], "capF", "capT")
        for t in range(3):
            for gl in range(2):
                c = 16 * gl + (0, 8, 40)[t]
                cp(T.capD[:, 16 * t + gl:16 * t + 16:2], T.capT[:, c:c + 8], "capT", "capD%d%d" % (t, gl))

    def swap(l, r, rhs4, b0, h, st, sp):
        for k in range(4):
            mm(pie[h][:, 0:4, k // 2, :], l[:, 128 * k:128 * k + 128], rhs4[:, b0 + 4 * h:b0 + 4 * h + 4, k % 2, :], st and k == 0, sp and k == 3, r, "pie%d" % h)

    def evac(h):
        act(T.PIE[:, 128 * h:128 * h + 128], pie[h][:, 0:4], F.Identity, "pie%d c9" % h, "PIE%d" % h, col(9))

    def gx(eng, t, u, n):
        out = Xb[t][:, 512 * u:512 * (u + n)]
        src = T.L[:, :].indirect(T.tile[:, 256 * t + 32 * u:256 * t + 32 * (u + n)])
        r = "L Lpad tile%d" % t
        if eng == "V": ts(out, src, XS, A.mult, r, Xu(t, u, n))
        else: act(out, src, F.Copy, r, Xu(t, u, n), 0.0, XS)

    def tx(t, p):
        o = 1024 * p + (16 if p >= 2 else 0)
        tr(T.XT[:, o:o + 1024], Xb[t][:, 1024 * p:1024 * p + 1024], Xu(t, 2 * p, 2), "XT%d" % p)

    def zmm(t, h):
        if h == 0:
            mm(T.zp[:, 0:8], T.If[:, :], T.offS[:, :], True, False, "If offS", "zp")
        if h == 0 and t == 2:
            mm(T.zp[:, 0:8], T.If[:, :], T.Z[:, rng(2)], False, False, "If Z", "zp")
        for k in range(32):
            mm(T.zp[:, 4 * h:4 * h + 4, k // 16, :], T.Iz[:, :], Xb[t][:, 2048 * h + k:2048 * h + 2048:32], False, h == 1 and k == 31, "Iz" + Xu(t, 4 * h, 4), "zp")

    def marks():
        for j in (1, 2):
            act(T.DF[:, rng(j)], T.seg[:, :], F.Sigmoid, "seg", "DF", -1000.0, 0.0)
        act(T.Pb[:, :], T.Pf[:, :], F.Copy, "Pf0 Pf1 Pf2 Pf3", "Pb", 0.0, 2.0 ** 26)

    def consts_b():
        ts(T.Woh[:, :], T.u17[:, :], col(1), A.is_equal, "u17 pF", "Woh")
        ts2(T.s1[:, :], T.u17[:, :], col(1), 1.0, A.subtract, A.is_equal, "u17 pF", "s1")
        ts2(T.d17[:, 16:17], col(1), 15.0, 2.0 ** 22, A.is_lt, A.mult, "pF", "d17a")
        ts(T.s2[:, :], T.Woh[:, :], -2.0, A.mult, "Woh", "s2")
        tt(T.d17[:, 17:33], T.Woh[:, 0:16], T.s1[:, 0:16], A.subtract, "Woh s1", "d17b")
        tt(T.dE[:, 17:34], T.s1[:, :], T.s2[:, :], A.add, "s1 s2", "dE1")
        ts(T.d17[:, 0:16], T.d17[:, 17:33], 2.0 ** 22, A.mult, "d17a d17b", "d17 d17b")
        ts(T.dE[:, 0:17], T.dE[:, 17:34], 4096.0, A.mult, "dE1", "dE dE1")
        ms(T.P2[:, :, 16], 0.0, "P2pad")
        ts(T.cTP[:, 16:272:17], T.dum[:, :], col(1), A.add, "dum pF", "cTP")

    def offers(t, src, sn):
        tr(T.ZT[:, :], src, sn, "ZT")
        scan(T.M1[:, :], T.seg[:, :], T.ZT[:, :], 0.0, A.add, A.min, "seg ZT", "M1")
        tt(T.k1[:, :], T.M1[:, 15:256:16], T.capD[:, 16 * t:16 * t + 16], A.min, "M1 capD%d0 capD%d1" % (t, t), "k1")
        ts(T.k2[:, :], T.k1[:, :], 4095, A.bitwise_and, "k1", "k2")
        cp(T.o1[:, :], T.k2[:, :], "k2", "o1")
        for h in range(2):
            tt(T.K2E[:, 128 * h:128 * h + 128], T.XT[:, 2064 * h:2064 * h + 2064].indirect(T.o1[:, 8 * h:8 * h + 8]), T.PIE[:, 128 * h:128 * h + 128], A.add,
               "XT%d XT%d XTpad%d o1 PIE%d" % (2 * h, 2 * h + 1, h, h), "K2E%d" % h)
        tr(T.ZT[:, :], T.K2E[:, :], "K2E0 K2E1", "ZT")
        scan(T.M1[:, :], T.seg[:, :], T.ZT[:, :], 0.0, A.add, A.min, "seg ZT", "M1")
        ts(T.KI[:, :], T.M1[:, 15:256:16], NOOFF, A.min, "M1", "KI")
        ts(T.EI[:, 0:16], T.KI[:, :], 8191, A.bitwise_and, "KI", "EI0")
        ts2(T.EI[:, 16:32], T.KI[:, :], 8191, 1, A.bitwise_and, A.arith_shift_right, "KI", "EI1")
        m = T.msg[:, 32 * t:32 * t + 32]
        cp(m, T.EI[:, :], "EI0 EI1", "msg%d" % t)
        send(T.mins[:, 32 * t:32 * t + 32], m, "arr%d" % t, T.cores[(rank + t + 1) % N], "msg%d" % t)
        ts2(T.iI[:, :], T.KI[:, :], 13, 15, A.arith_shift_right, A.bitwise_and, "KI", "iI")
        cp(T.iT[:, :], T.iI[:, :], "iI", "iT")

    def own(t):
        if t < 2: act(T.ohb[:, :], T.Woh[:, 0:16].indirect(T.iT[:, :]), F.Identity, "Woh iT", "ohb", XS, -XS)
        else: act(T.Q1[:, :], T.Woh[:, 0:16].indirect(T.iT[:, :]), F.Identity, "Woh iT", "Q1", 2.0, -1.0)

    def over(t):
        act(T.ov[:, rng(t)], T.W[:, :].indirect(T.msg[:, 32 * t:32 * t + 16]), F.Sign, "W msg%d" % t, "ov%d" % t, 4097.0, -1.0)

    def acc(t): return T.Wacc[:, :].indirect(T.rin[:, 16 * t:16 * t + 16])

    def answer(t):
        arrive("rin%d" % t, "rep%d" % t, T.cores[(rank + t + 1) % N])
        if t < 2:
            act(T.accb[:, :], acc(t), F.Copy, "Wacc rin%d" % t, "accb", 0.0, -XS)
            mm(T.valB[:, 0:256], T.Iz[:, :], T.ohb[:, :], True, False, "Iz ohb", "valB")
            mm(T.valB[:, 0:256], T.Iz[:, :], T.accb[:, :], False, True, "Iz accb", "valB")
        else:
            tt(T.LFo[:, :], acc(t), T.Q2[:, :], A.is_lt, "Wacc rin2 Q2", "LFo")
            dma("Y", "dO2", T.left[:, rng(t)], T.LFo[:, :], "LFo")

    def taken(t):
        tt(T.Ai[:, rng(t)], T.Ai[:, rng(t)], T.valB[:, 0:256], A.max, "valB" + An(t), An(t))

    def said(t):
        tt(T.sd[:, rng(t)], acc(t), T.ov[:, rng(t)], A.add, "Wacc rin%d ov%d" % (t, t), "sd%d" % t)

    def verdict(t, fill_rep, fill_val, fill_s, fill_s2):
        mm(T.hA[:, 0:272], T.B32[:, :], c1, True, False, "B32 cst", "hA")
        mm(T.hB[:, 0:272], T.B32[:, :], c3, True, False, "B32 cst", "hB")
        mm(T.TP[:, 0:272], T.If[:, :], T.cTP[:, :], True, False, "If cTP", "TP")
        mn = " min%d " % t
        arrive(mn, "arr%d" % t, T.cores[(rank - t - 1) % N])
        oT, kT = T.mins[:, 32 * t:32 * t + 16], T.mins[:, 32 * t + 16:32 * t + 32]
        cp(T.cand[:, :], T.Bi[:, :].indirect(kT), "B Bpad" + mn, "cand")
        act(T.oppB[:, :], T.W[:, :].indirect(oT), F.Copy, "W" + mn, "oppB")
        ts2(T.cn[:, :], T.cand[:, :], -1.0, 2048.0, A.mult, A.add, "cand", "cn")
        fill_rep()
        for k in range(8):
            e = slice(512 * k, 512 * k + 512)
            act(T.rep[:, e], T.oppB[:, :].indirect(T.colc[:, 32 * k:32 * k + 32]), F.Copy, "oppB colc", "rep%d" % k)
            tt(T.eq[:, e], T.Ai[:, :].indirect(T.cand[:, 32 * k:32 * k + 32]), T.rep[:, e], A.is_equal, Aall + "cand rep%d" % k, "eq%d" % k)
            if k % 2:
                b = k // 2
                for j in range(16):
                    mm((T.valB if b == 3 else T.valA)[:, 64 * b:64 * b + 64], T.Fj[:, 128 * j:128 * j + 128], T.eq[:, 1024 * b + j:1024 * b + 1024:16],
                       j == 0, j == 15, "Fj%d eq%d eq%d" % (j, k - 1, k), "valB" if b == 3 else "valA")
        fill_s()
        for v, vn, a, b in ((T.valA, "valA", 0, 12), (T.valB, "valB", 12, 16)):
            tt(T.P1[:, 16 * a:16 * b], v[:, 16 * a:16 * b], T.cn[:, 16 * a:16 * b], A.min, vn + " cn", "P1" + vn)
            ts(T.P2[:, a:b, 0:16], T.P1[:, 16 * a:16 * b], 0.0, A.max, "P1" + vn, "P2" + vn)
            mm(T.hA[:, 17 * a:17 * b], T.NBO[:, :], T.P2[:, a:b, :], False, a > 0, "NBO P2pad P2" + vn, "hA")
            if a == 0:
                mm(T.hB[:, 0:204], T.NBO[:, :], T.P2[:, a:b, :], False, False, "NBO P2" + vn, "hB")
                if t < 2:
                    ts2(T.s1[:, 0:16], kT, 4.0, 1.0, A.mult, A.add, mn, "s1")
                    cp(T.s2[:, 0:16], oT, mn, "s2")
                    tt(T.dum[:, :], T.s1[:, 0:16], T.s2[:, 0:16], A.subtract, "s1 s2", "dum")
                fill_val()
        if t < 2:
            cp(T.oL[:, :], T.dum[:, :], "dum", "oL")
            act(T.Lo[:, :], T.L[:, :].indirect(T.oL[:, :]), F.Copy, "L Lpad oL", "Lo")
        fill_s2()
        mm(T.hB[:, 204:272], T.NBO[:, :], T.P2[:, 12:16, :], False, True, "NBO P2valB", "hB")
        mm(T.TP[:, 0:272], T.NBO[:, :], T.P2[:, :, :], False, False, "NBO P2valA P2valB", "TP")
        scan(T.E[:, :], T.dE[:, :], T.hA[:, 0:272], -20000.0, A.add, A.max, "dE hA", "E")
        cp(T.h16[:, :], T.hA[:, 0:272], "hA", "h16")
        tt(T.eqd[:, 0:272], T.E[:, :], T.hB[:, 0:272], A.is_equal, "E hB", "edd")
        mm(T.TP[:, 0:272], BO, T.eqd[:, 0:272], False, False, "BO edd", "TP")
        o = 272
        for q in range(15):
            n = 17 * (15 - q)
            ts2(T.eqd[:, o:o + n], T.h16[:, 272 - n:272], 4096.0, T.E[:, 17 * q + 16:17 * q + 17], A.add, A.is_equal, "h16 E", "ed%d" % q)
            mm(T.TP[:, 272 - n:272], BO, T.eqd[:, o:o + n], False, q == 14, "BO ed%d" % q, "TP")
            o += n
        ts(T.hT[:, :], T.E[:, 16:272:17], 4096.0, A.subtract, "E", "hT")
        tt(T.eqm[:, :], T.Ai[:, :].indirect(T.hT[:, :]), T.oppB[:, :], A.is_equal if t < 2 else A.not_equal, Aall + "hT oppB", "eqm")
        if t < 2:
            act(T.cZ[:, :], T.Z[:, :].indirect(T.hT[:, :]), F.Copy, "Z hT", "cZ")
            mm(T.valA[:, 0:256], BO, T.eqm[:, :], True, True, "BO eqm", "valA")
            act(T.xs[:, :], T.eqm[:, :], F.Identity, "eqm", "xs", -1000.0, 2000.0)
        else:
            act(T.cL[:, :], T.LF[:, :].indirect(T.hT[:, :]), F.Copy, "LF hT", "cL")
        scan(T.S2[:, :], T.d17[:, :], T.TP[:, 0:272], 0.0, A.add, A.min, "d17 TP", "S2")
        off, rn = T.rout[:, 16 * t:16 * t + 16], " rout%d " % t
        cp(off, T.S2[:, 16:272:17], "S2", rn)
        send(T.rin[:, 16 * t:16 * t + 16], off, "rep%d" % t, T.cores[(rank - t - 1) % N], rn)
        if t < 2:
            tt(T.kL[:, :], T.valA[:, 0:256], T.Lo[:, :], A.mult, "valA Lo", "kL")
            tt(T.Z[:, :].indirect(off), T.cZ[:, :], T.kL[:, :], A.add, rn + "cZ kL", "Z")
            op("S", lambda q: q.activation(T.DF[:, :].indirect(off), T.xs[:, :], F.Sigmoid), rn + "xs", "DF")
            for h in range(2):
                c = 256 * (t + 1) + 128 * h
                act(T.DFb[:, 8 * t + 4 * h:8 * t + 4 * h + 4], T.DF[:, c:c + 128], F.Copy, "DF", "DFb%d%d" % (t, h))
                swap(T.Pb, "Pb DFb%d%d" % (t, h), T.DFb, 8 * t, h, False, True)
            evac(0); evac(1)
            act(T.e4[:, :], T.eqm[:, :], F.Copy, "eqm", "e4", 0.0, 4096.0)
            if t == 0:
                act(T.DFb[:, 16:24], T.DF[:, 512:768], F.Copy, "DF", "DFb2")
        else:
            tt(T.LF[:, :].indirect(off), T.cL[:, :], T.eqm[:, :], A.mult, rn + "cL eqm", "LF")

    def change(t):
        tt(T.nA[:, :], T.Ai[:, :].indirect(T.hT[:, :]), T.e4[:, :], A.max, Aall + "hT e4", "nA")
        cp(T.Ai[:, :].indirect(T.rout[:, 16 * t:16 * t + 16]), T.nA[:, :], "nA rout%d" % t, Aall)

    def zbase(t):
        act(T.Z[:, rng(t)], T.zp[:, 0:8], F.Copy, "zp", "Z")

    def lf(a, b):
        ts(T.LF[:, a:b], T.Ai[:, a:b], 4096.0, A.is_lt, Aall, "LF")

    prep_tile(0)
    ts2(T.Iz[:, :], T.dif[:, :], 0.0, 1.0 / 32, A.is_equal, A.mult, "dif", "Iz")
    ts(T.If[:, :], T.dif[:, :], 0.0, A.is_equal, "dif", "If")
    ts(T.offS[:, 128:256], T.offS[:, 0:128], col(2), A.add, "offS pF", "offS2")
    cp(T.offS[:, 0:128], T.offS[:, 128:256], "offS2", "offS")
    for k in range(4):
        ts2(T.Pf[:, 128 * k:128 * k + 128], T.dif[:, :], 16.0 * (k // 2 - k % 2), col(3 if k // 2 else 8), A.is_equal, A.mult, "dif pF c8", "Pf%d" % k)
    prep_pos(0)
    for h in range(2):
        swap(T.Pf, "Pf0 Pf1 Pf2 Pf3 Of0", T.Of4, 0, h, True, True)
    prep_cap()
    cp(T.colc[:, :], T.colf[:, :], "colf", "colc")
    gx("V", 0, 0, 2); gx("S", 0, 2, 2); zmm(0, 0)
    gx("V", 0, 4, 1); gx("S", 0, 5, 3); zmm(0, 1)
    evac(0); evac(1)
    tx(0, 0); tx(0, 1)
    prep_tile(1)
    consts_b()
    tx(0, 2); tx(0, 3)
    for p in range(4):
        gx("S", 1, 2 * p, 2)
    offers(0, T.zp[:, 0:8], "zp")
    for j in range(12, 16):
        gcp(T.Fj[:, 128 * j:128 * j + 128], T.Fv[:, :, 15 - j:31 - j], 128, "Fv", "Fj%d" % j)
    for n in (1, 2, 4, 8):
        gcp(T.dE[:, 17 * n:34 * n], T.dE[:, 0:17 * n], 17 * n, "dE", "dE")
        gcp(T.d17[:, 17 * n:34 * n], T.d17[:, 0:17 * n], 17 * n, "d17", "d17")
    iota(T.LF[:, 2048:2320], [[0, 272]], 0, 0, "LF")
    iota(T.Z[:, 1024:2320], [[0, 1296]], 0, 0, "Z")
    iota(T.Wacc[:, 0:2048], [[0, 2048]], 1, 0, "Wacc")
    iota(T.Wacc[:, 2048:2320], [[0, 272]], 0, 0, "Wacc1")
    lastw["Wacc"] = lastw["Wacc1"]
    zmm(1, 0); zmm(1, 1)
    ts(T.NBO[:, :], BO, -1.0 / 4096, A.mult, "BO", "NBO")
    for j in range(12):
        cp(T.Fj[:, 128 * j:128 * j + 128], T.Fv[:, :, 15 - j:31 - j], "Fv", "Fj%d" % j)
    ts(T.B32[:, :], BO, 1.0 / 32, A.mult, "BO", "B32")
    prep_tile(2)
    prep_pos(1)
    for h in range(2):
        swap(T.Pf, "Of1", T.Of4, 8, h, True, False)
    tx(1, 0); tx(1, 1); tx(1, 2)
    verdict(0, lambda: tx(1, 3), lambda: None, lambda: (marks(), zbase(1), own(0), gx("S", 2, 0, 2)), lambda: gx("S", 2, 2, 1))
    offers(1, T.Z[:, 256:512], "Z")
    gx("S", 2, 3, 1)
    answer(0)
    gx("S", 2, 4, 2); gx("S", 2, 6, 2)
    prep_pos(2)
    zmm(2, 0)
    for h in range(2):
        swap(T.Pf, "Of2", T.Of4, 16, h, True, False)
        swap(T.Pb, "Pb DFb2", T.DFb, 16, h, False, False)
    zmm(2, 1)
    change(0)
    tx(2, 0); tx(2, 1); tx(2, 2)
    taken(0)
    verdict(1, lambda: tx(2, 3), lambda: None, lambda: (zbase(2), own(1)), lambda: None)
    offers(2, T.Z[:, 512:768], "Z")
    change(1)
    answer(1)
    lf(768, 2048)
    taken(1)
    verdict(2, lambda: lf(0, 512), lambda: lf(512, 768), lambda: (own(2), over(0), over(1), over(2)), lambda: None)
    dma("Y", "dO0", T.left[:, 768:2048], T.LF[:, 768:2048], "LF")
    dma("S", "dO1", T.left[:, 0:512], T.LF[:, 0:512], "LF")
    tt(T.Q2[:, :], T.LF[:, 512:768], T.Q1[:, :], A.mult, "LF Q1", "Q2")
    said(0); said(1)
    dma("Y", "dS0", T.said[:, 0:512], T.sd[0:128:16, 0:512], "sd0 sd1")
    answer(2)
    said(2)
    dma("S", "dS1", T.said[:, 512:768], T.sd[0:128:16, 512:768], "sd2")

    known = {e: {} for e in Q}
    for o in ops:
        o["key"] = o["sem"] or o["eng"]
        o["clock"] = {}
        if o["eng"] == "X":
            continue
        kn = known[o["eng"]]
        for d in sorted(o["deps"], reverse=True):
            p = ops[d]
            if p["sem"] == "remote" or kn.get(p["key"], -1) >= d:
                continue
            p["need"] = True
            o["waits"].append(d)
            kn[p["key"]] = d
            for a, b in p["clock"].items():
                kn[a] = max(kn.get(a, -1), b)
        o["clock"] = dict(kn)
    count = {e: 0 for e in "VSPG"}
    for o in ops:
        if o["sem"] is None and o["need"]:
            count[o["eng"]] += 1
            o["cnt"] = count[o["eng"]]
    for o in ops:
        if o["eng"] == "X":
            continue
        q = Q[o["eng"]]
        for d in o["waits"]:
            q.wait_ge(T.sem[ops[d]["sem"] or "s" + ops[d]["eng"]], ops[d]["cnt"])
        ins = o["fn"](q)
        if o["sem"] is None:
            if o["need"]:
                ins.then_inc(T.sem["s" + o["eng"]], 1)
        elif o["sem"] != "remote":
            ins.then_inc(T.sem[o["sem"]], 16)
    g.wait_ge(T.sem.sent, sent[0])
    for s in DMAS:
        g.sync.wait_ge(T.sem[s], 16)
